import numpy as np, ml_dtypes
CORES = [6,15,38,47]
N = 4
BF = ml_dtypes.bfloat16
S, M, CAP, L = 1024, 768, 352, 4
F = 16 // N
def tries(rng, same=False, few=False):
    kid = np.zeros((N, 8, M, 16), np.int32); words = {}; deep = {}
    tid = (rng.integers(1, 65536, (N, 8, M)) * (rng.random((N, 8, M)) < (0.0625 if few else 0.5))).astype(np.int32)
    for q in range(N):
        for g in range(8):
            no = [0, 1] + (2 + rng.permutation(M - 2)).tolist(); pl = rng.random(M).tolist(); cl = rng.integers(0, 16, M).tolist()
            k = kid[q, g]; w = {1: []}; up = []; m = 2; deep[q, g] = []
            for c in (q * F + rng.permutation(F)).tolist()[:1 if few else F]:
                p = 1
                for d in range(L):
                    e = c if d == 0 or same else cl[m]
                    k[no[p], e] = no[m]; w[m] = w[p] + [e]
                    if d < L - 1: up.append(m)
                    p = m; m += 1
                tid[q, g, no[p]] = rng.integers(1, 65536); deep[q, g].append(w[p])
            for m in range(m, M):
                p = up[int(pl[m] * len(up))]; e = cl[m]
                if k[no[p], e]: continue
                k[no[p], e] = no[m]; w[m] = w[p] + [e]
                if len(w[m]) < L: up.append(m)
            words[q, g] = [v for v in w.values() if v]
    tid[:, :, 0] = 0
    return kid.reshape(N, 8, 16 * M), tid, words, deep
def strings(rng, words):
    s = np.zeros((8, N * S), np.int64)
    for g in range(8):
        qs = rng.integers(0, N, N * S).tolist(); ms = rng.random(N * S).tolist(); a = []; i = 0
        while len(a) < N * S:
            v = words[qs[i], g]; a += v[int(ms[i] * len(v))]; i += 1
        s[g] = a[:N * S]
    return np.where(rng.random(s.shape) < 0.1, rng.integers(0, 16, s.shape), s)
def plant(rng, s, deep):
    keep = np.zeros(s.shape, bool)
    for r in range(N):
        for g in range(8):
            v = deep[int(rng.integers(0, N)), g]; j = (r * S + S - 1 - g % (L - 1) + np.arange(L)) % (N * S)
            s[g, j] = v[int(rng.integers(0, len(v)))]; keep[g, j] = True
    return keep
def fit(rng, s, keep, full=False):
    s = s.reshape(8, N, S).transpose(1, 0, 2).astype(np.int32); keep = keep.reshape(8, N, S).transpose(1, 0, 2)
    a, b = int(rng.integers(0, N)), int(rng.integers(0, 8))
    for r in range(N):
        for g in range(8):
            e = s[r, g]; own = e // F; have = np.bincount(own, minlength=N); low = np.bincount(own[keep[r, g]], minlength=N)
            o = rng.permutation(N); i = np.flatnonzero((o == a) if full and g == b else (o != r))[0]; o[[0, i]] = o[[i, 0]]
            want = low.copy() if full else np.minimum(have, CAP)
            if full or (r, g) == (a, b): want[o[0]] = CAP
            for q in np.roll(o, -1): want[q] = min(max(int(want[q]) + S - int(np.sum(want)), int(low[q])), CAP)
            sur = np.concatenate([rng.permutation(np.flatnonzero((own == q) & ~keep[r, g]))[:max(int(have[q] - want[q]), 0)] for q in range(N)])
            need = np.repeat(np.arange(N), np.maximum(want - have, 0))
            e[sur] = need * F + rng.integers(0, F, len(need))
    return np.ascontiguousarray(s)
def setup_inputs(rng):
    kid, tid, words, deep = tries(rng); s = strings(rng, words); keep = plant(rng, s, deep)
    return {"lett": fit(rng, s, keep), "kid": kid, "tid": tid}
def setup_inputs_full(rng):
    kid, tid, words, deep = tries(rng); s = strings(rng, words)
    lett = fit(rng, s, np.zeros(s.shape, bool), True)
    assert np.sum((lett // F)[..., None] == np.arange(N), axis=2).min(axis=0).max() == CAP
    return {"lett": lett, "kid": kid, "tid": tid}
def setup_inputs_runs(rng):
    kid, tid, words, deep = tries(rng, same=True)
    s = np.stack([np.repeat(rng.integers(0, 16, N * S), rng.integers(1, 13, N * S))[:N * S] for g in range(8)]); keep = plant(rng, s, deep)
    return {"lett": fit(rng, s, keep), "kid": kid, "tid": tid}
def setup_inputs_few(rng):
    kid, tid, words, deep = tries(rng, few=True); s = strings(rng, words); keep = plant(rng, s, deep)
    return {"lett": fit(rng, s, keep), "kid": kid, "tid": tid}
def setup_inputs_spread(rng):
    kid = (rng.integers(0, M, (N, 8, M, 16)) * (rng.random((N, 8, M, 16)) > 0.125)).astype(np.int32)
    kid[:, :, 0] = 0; kid[:, :, 1] *= (np.arange(16) // F == np.arange(N)[:, None])[:, None, :]
    tid = (rng.integers(0, 65536, (N, 8, M)) * (rng.random((N, 8, M)) < 0.3)).astype(np.int32); tid[:, :, 0] = 0; tid[:, :, M - 1] = 65535
    s = np.minimum(np.floor(rng.random((8, N * S)) ** 2 * 16), 15).astype(np.int64)
    return {"lett": fit(rng, s, np.zeros(s.shape, bool)), "kid": kid.reshape(N, 8, 16 * M), "tid": tid}
def check_inputs(d):
    bad = []; s, kid, tid = d["lett"], d["kid"], d["tid"]
    if s.min() < 0 or s.max() > 15: bad.append("letters")
    if ((s // F)[..., None] == np.arange(N)).sum(2).max() > CAP: bad.append("slots")
    if kid.min() < 0 or kid.max() >= M: bad.append("children")
    if kid[:, :, :16].any() or tid[:, :, 0].any(): bad.append("node 0")
    if (kid[:, :, 16:32] * (np.arange(16) // F != np.arange(N)[:, None])[:, None, :]).any(): bad.append("roots")
    if tid.min() < 0 or tid.max() > 65535: bad.append("ids")
    return bad
def reference(lett, kid, tid):
    s = np.concatenate(list(lett), axis=1).astype(np.int64)
    own = s // F; g = np.arange(8)[:, None]; node = np.ones(s.shape, np.int64); yl = np.zeros(s.shape, np.int64); yi = np.zeros(s.shape, np.int64)
    for k in range(L):
        node = kid[own, g, 16 * node + np.roll(s, -k, axis=1)].astype(np.int64)
        t = tid[own, g, node]
        yl = np.where(t > 0, k + 1, yl); yi = np.where(t > 0, t, yi)
    yl = np.ascontiguousarray(yl.reshape(8, N, S).transpose(1, 0, 2)); yi = np.ascontiguousarray(yi.reshape(8, N, S).transpose(1, 0, 2))
    return {"ylen": yl.astype(np.float32), "yid": yi.astype(np.float32)}

@@ -1,0 +1,369 @@
+import numpy as np
+from concourse.bass import DstId, RemoteDMATransfer
+from concourse.mybir import AluOpType as A, AxisListType, ActivationFunctionType as F
+
+NR = 4
+M = 768
+HF = "float16"
+BF = "bfloat16"
+F32 = "float32"
+I32 = "int32"
+U16 = "uint16"
+
+
+def sb(cols, dtype):
+    return ("sbuf", [128] + (cols if isinstance(cols, list) else [cols]), dtype)
+
+
+SCRATCH = {
+    "lbuf": ("dram", [4, 128, 16], I32), "lin": ("dram", [4, 128, 16], I32),
+    "tbuf": ("dram", [4, 128, 12], I32), "tin": ("dram", [4, 128, 12], I32),
+    "kx": sb([12, 64], I32), "kh": sb([6, 128], HF), "ks": sb(768, HF), "kin": sb(768, HF),
+    "win": sb(3072, F32), "tw": sb(3072, BF), "nw": sb(256, F32),
+    "ht": sb(96, I32), "hhi": sb(96, I32), "hlo": sb(96, I32), "hb": sb(288, BF),
+    "lu": sb(1040, I32), "uh": sb(1040, BF), "em": sb(1040, BF),
+    "pi": sb(1, I32), "pci": sb(1, I32), "pgi": sb(1, I32), "poi": sb(1, I32),
+    "kf": sb(1, F32), "pcf": sb(1, F32), "k16": sb(1, F32), "own1": sb(1, F32), "k168": sb(1, F32),
+    "imk": sb(128, F32), "ix": sb(143, F32), "mi": sb(128, I32), "own16": sb(16, F32), "expi": sb(16, I32),
+    "expu": sb(16, U16), "ma": sb(128, I32), "mb": sb(128, I32), "mc": sb(128, F32), "fm": sb(128, F32),
+    "pm": sb(128, I32), "e8": sb(128, BF), "f8": sb(143, BF), "f8s": sb(143, BF),
+    "r0": sb(128, HF), "r1": sb(128, HF), "r2": sb(128, HF), "r3": sb(128, HF),
+    "ih": sb(128, HF), "ib": sb(128, BF), "shb": sb(128, BF), "t1h": sb(143, HF),
+    "wa": sb(1, F32), "wb": sb(1, F32), "wab": sb(1, F32), "wf": sb(1, F32), "wg": sb(1, F32), "wh": sb(1, F32),
+    "wi": sb(1, F32), "wj": sb(1, F32),
+    "w1": sb(1, F32), "w2": sb(1, F32), "w3": sb(1, F32), "w4": sb(1, F32),
+    "tw1": sb(143, BF), "tw2": sb(143, BF), "tw3": sb(143, BF), "tw4": sb(143, BF),
+    "ci": sb(64, I32), "cu": sb(64, U16), "oi": sb(64, I32), "ownl": sb(64, HF),
+    "n1s": sb(1, F32), "n1u": sb(2, U16), "n2f": sb(16, F32), "n2u": sb(16, U16), "n3u": sb(64, U16), "n4u": sb(64, U16),
+    "p3": sb(1024, HF), "p4": sb(1024, HF),
+    "g1": sb(16, BF), "g1e": sb(256, BF), "g2": sb(256, BF), "g12": sb(256, BF),
+    "i12": sb(1024, BF), "i3": sb(1024, BF), "i4": sb(1024, BF),
+    "b1": sb(64, F32), "b2": sb(64, F32), "b3": sb(64, F32),
+    "res": sb(256, I32), "li": sb(256, I32), "ii": sb(256, I32), "yl": sb(256, F32), "yi": sb(256, F32),
+}
+for _i in range(8):
+    SCRATCH["ps%d" % _i] = ("psum", [128, 512], F32)
+SEMAPHORES = (["cv", "ca", "ct", "cg", "sl", "st", "sk", "sr"] + ["r%s%d" % (x, i) for x in "ltkr" for i in range(NR)]
+              + ["d%d" % i for i in range(48)])
+
+
+def shares(topo, src, dsts):
+    far = [d for d in dsts if not topo.mates(topo.chip(src), topo.chip(d))
+           and not topo.same_plane(topo.chip(src), topo.chip(d))]
+    order = far + [d for d in dsts if d not in far]
+    out = {}
+    at = 0
+    for i, d in enumerate(order):
+        e = topo.engines(src, d)
+        n = len(e) // 2 if i == 0 else len(e) // 4
+        out[d] = e[at:at + n]
+        at += n
+    return out
+
+
+def bits(engines):
+    return sum(1 << e for e in engines)
+
+
+def rank_program(g, core, T, topo):
+    me = T.rank_of(core)
+    if me is None:
+        return
+    cores = list(T.cores)
+    others = [q for q in range(NR) if q != me]
+    q_of = {"g": g, "v": g.vector, "a": g.scalar, "t": g.tensor, "s": g.sync}
+    csem = {"g": "cg", "v": "cv", "a": "ca", "t": "ct"}
+    total = {}
+    waited = {}
+    seen = {}
+    lastw = {}
+    reads = {}
+    ndma = [0]
+
+    def wait(q, evs):
+        most = {}
+        for s, v in evs:
+            most[s] = max(v, most.get(s, 0))
+        for s in most:
+            if waited.get((q, s), 0) < most[s]:
+                q_of[q].wait_ge(T.sem[s], most[s])
+                waited[(q, s)] = most[s]
+                seen[s] = max(seen.get(s, 0), most[s])
+
+    def deps(q, R, W):
+        own = csem.get(q)
+        evs = []
+        for k in R:
+            evs += lastw.get(k, [])
+        for k in W:
+            evs += [e for e in lastw.get(k, []) + reads.get(k, []) if e[0] != own]
+        wait(q, evs)
+
+    def note(ev, R, W):
+        for k in W:
+            lastw[k] = [ev]
+            reads[k] = []
+        for k in R:
+            reads.setdefault(k, []).append(ev)
+
+    def comp(q, R, W, calls):
+        deps(q, R, W)
+        s = csem[q]
+        for c in (calls if isinstance(calls, list) else [calls]):
+            c().then_inc(T.sem[s], 1)
+            total[s] = total.get(s, 0) + 1
+        note((s, total[s]), R, W)
+
+    def V(R, W, *calls):
+        comp("v", R, W, list(calls))
+
+    def act(R, W, o, i):
+        comp("a", R, W, lambda: g.scalar.activation(o, i, F.Copy))
+
+    def dma(q, out, in_, R, W):
+        deps(q, R, W)
+        s = "d%d" % ndma[0]
+        ndma[0] += 1
+        q_of[q].dma_start(out, in_).then_inc(T.sem[s], 16)
+        total[s] = 16
+        note((s, 16), R, W)
+
+    def arrive(s, n, keys):
+        total[s] = total.get(s, 0) + n
+        for k in keys:
+            lastw[k] = [(s, total[s])]
+
+    def dst(d):
+        rid, pid, _ = topo.addr(d)
+        return DstId(rid=rid, pnc=pid)
+
+    mine = shares(topo, core, [cores[q] for q in others])
+
+    def send(rsem, lsem, src_of, out, R):
+        deps("g", R, [])
+        tr = [RemoteDMATransfer(dst_ids=[dst(cores[q])], dma_engine_mask=bits(mine[cores[q]]),
+                                remote_sem=T.sem["r%s%d" % (rsem, me)], src=src_of(q), dst=out) for q in others]
+        g.remote_dma_fused(tr, local_sem=T.sem[lsem])
+        total[lsem] = sum(len(mine[cores[q]]) for q in others)
+
+    def got(q):
+        return len(shares(topo, cores[q], [c for c in cores if c != cores[q]])[core])
+
+    v = g.vector
+    pe = g.tensor
+    ps = [T["ps%d" % i] for i in range(8)]
+
+    dma("s", T.lbuf[:], T.lett[:], [], ["lbuf"])
+    dma("a", T.kx[:, 0:6, :], T.kid[0::2, :], [], ["kx0"])
+    dma("s", T.kx[:, 6:12, :], T.kid[1::2, :], [], ["kx1"])
+    dma("a", T.tbuf[:], T.tid[:], [], ["tbuf"])
+    dma("s", T.lin[me], T.lett[2 * me:2 * me + 2, :], [], ["lin%d" % me])
+    dma("a", T.tin[me], T.tid[2 * me:2 * me + 2, :], [], ["tin%d" % me])
+
+    comp("g", [], ["pi"], lambda: g.iota(T.pi[:], [[1, 1]], 0, 1))
+    comp("g", [], ["imk"], lambda: g.iota(T.imk[:], [[1, 128]], 0, -1, allow_small_or_imprecise_dtypes=True))
+    comp("g", [], ["mi"], lambda: g.iota(T.mi[:], [[1, 128]], 0, 0))
+    comp("g", [], ["ix"], lambda: g.iota(T.ix[:], [[1, 143]], 0, 0, allow_small_or_imprecise_dtypes=True))
+    comp("g", [], ["own16"], lambda: g.iota(T.own16[:], [[M, 4], [0, 4]], 0, 0, allow_small_or_imprecise_dtypes=True))
+    comp("g", [], ["expi"], lambda: g.iota(T.expi[:], [[1, 16]], 0, 0))
+
+    send("l", "sl", lambda q: T.lbuf[q], T.lin[me], ["lbuf"])
+    send("t", "st", lambda q: T.tbuf[q], T.tin[me], ["tbuf"])
+    for q in others:
+        arrive("rl%d" % q, got(q), ["lin%d" % q])
+        arrive("rt%d" % q, got(q), ["tin%d" % q])
+
+    V(["imk"], ["ih"], lambda: v.tensor_scalar(T.ih[:], T.imk[:], 0.0, None, A.is_equal))
+    V(["pi"], ["pci"], lambda: v.tensor_scalar(T.pci[:], T.pi[:], 15, None, A.bitwise_and))
+    V(["pi"], ["pgi"], lambda: v.tensor_scalar(T.pgi[:], T.pi[:], 112, None, A.bitwise_and))
+    V(["pi"], ["poi"], lambda: v.tensor_scalar(T.poi[:], T.pi[:], 12, None, A.bitwise_and))
+    V(["pi"], ["kf"], lambda: v.tensor_copy(T.kf[:], T.pi[:]))
+    V(["mi"], ["ma"], lambda: v.tensor_scalar(T.ma[:], T.mi[:], 15, None, A.bitwise_and))
+    V(["mi"], ["mb"], lambda: v.tensor_scalar(T.mb[:], T.mi[:], 16, None, A.bitwise_and))
+    V(["mi"], ["pm"], lambda: v.tensor_scalar(T.pm[0:8, :], T.mi[0:8, :], 4, None, A.arith_shift_right))
+    V(["pci"], ["pcf"], lambda: v.tensor_copy(T.pcf[:], T.pci[:]))
+    V(["pgi"], ["k16"], lambda: v.tensor_scalar(T.k16[:], T.pgi[:], 15.0, None, A.add))
+    V(["poi"], ["own1"], lambda: v.tensor_scalar(T.own1[:], T.poi[:], 192.0, None, A.mult))
+    V(["kf"], ["k168"], lambda: v.tensor_scalar(T.k168[0:8, :], T.kf[0:8, :], 16.0, 15.0, A.mult, A.add))
+    V(["mb"], ["mc"], lambda: v.tensor_scalar(T.mc[:], T.mb[:], 4.0, None, A.mult))
+    V(["pm", "kf"], ["e8"], lambda: v.tensor_scalar(T.e8[0:8, :], T.pm[0:8, :], T.kf[0:8, :], None, A.is_equal))
+    V(["mc", "ma"], ["fm"], lambda: v.tensor_tensor(T.fm[:], T.mc[:], T.ma[:], A.add))
+    V(["ix", "k168"], ["f8"], lambda: v.tensor_scalar(T.f8[0:8, :], T.ix[0:8, :], T.k168[0:8, :], None, A.is_equal))
+    V(["ix", "k168"], ["f8s"],
+      lambda: v.tensor_scalar(T.f8s[0:8, :], T.ix[0:8, :], T.k168[0:8, :], 16.0, A.is_equal, A.mult))
+    for n in range(4):
+        V(["fm", "kf"], ["r%d" % n],
+          lambda: v.tensor_scalar(T["r%d" % n][:], T.fm[:], T.kf[:], float(-16 * n), A.subtract, A.is_equal))
+
+    for la in range(2):
+        V(["kx%d" % la], ["kh%d" % la],
+          lambda: v.tensor_copy(T.kh[:, :, 64 * la:64 * la + 64], T.kx[:, 6 * la:6 * la + 6, :]))
+    for b in range(6):
+        comp("t", ["kh0", "kh1", "ih"], ["ps%d" % (b // 2)],
+             lambda: pe.matmul(ps[b // 2][:, 128 * (b % 2):128 * (b % 2) + 128], T.kh[:, b, :], T.ih[:], True, True))
+    for b in range(6):
+        V(["ps%d" % (b // 2)], ["ks%d" % b],
+          lambda: v.tensor_copy(T.ks[:, b::6], ps[b // 2][:, 128 * (b % 2):128 * (b % 2) + 128]))
+    ksk = ["ks%d" % b for b in range(6)]
+    send("k", "sk", lambda q: T.ks[:, 192 * q:192 * q + 192], T.kin[:, 192 * me:192 * me + 192], ksk)
+    for q in others:
+        arrive("rk%d" % q, got(q), ["kin%d" % q])
+
+    lins = ["lin%d" % q for q in range(4)]
+    tins = ["tin%d" % q for q in range(4)]
+    dma("s", T.lu[0:8, 0:1024], T.lin[:], lins, ["lua"])
+    dma("s", T.lu[0:6, 1024:1040], T.lin[1:4, 0::64, :], lins, ["lub"])
+    dma("s", T.lu[6:8, 1024:1040], T.lin[0, 0::64, :], lins, ["luc"])
+    for la in range(2):
+        dma("s", T.ht[32 * la:32 * la + 32, :], T.tin[:, 64 * la:64 * la + 64, :], tins, ["ht%d" % la])
+
+    V([], ["tw"], lambda: v.memset(T.tw[:], 0.0))
+    V(["ix", "k16"], ["t1h"], lambda: v.tensor_scalar(T.t1h[:], T.ix[:], T.k16[:], None, A.is_equal))
+    V(["imk"], ["ib"], lambda: v.tensor_scalar(T.ib[:], T.imk[:], 0.0, None, A.is_equal))
+    V(["imk"], ["shb"], lambda: v.tensor_scalar(T.shb[:], T.imk[:], 3.0, None, A.is_equal))
+    V(["expi"], ["expu"], lambda: v.tensor_copy(T.expu[:], T.expi[:]))
+    for nm, c, wt in (("wa", 0, 256.0), ("wb", 1, 1.0), ("wf", 2, 65536.0), ("wg", 3, 256.0), ("wh", 4, 1.0),
+                      ("wi", 5, 65536.0)):
+        V(["pcf"], [nm], lambda: v.tensor_scalar(T[nm][:], T.pcf[:], float(c), wt, A.is_equal, A.mult))
+    V(["wa", "wb"], ["wab"], lambda: v.tensor_tensor(T.wab[:], T.wa[:], T.wb[:], A.add))
+    V(["wg", "wh"], ["wj"], lambda: v.tensor_tensor(T.wj[:], T.wg[:], T.wh[:], A.add))
+
+    hts = ["ht0", "ht1"]
+    V(hts, ["hhi"], lambda: v.tensor_scalar(T.hhi[0:64, :], T.ht[0:64, :], 8, None, A.arith_shift_right))
+    V(hts, ["hlo"], lambda: v.tensor_scalar(T.hlo[0:64, :], T.ht[0:64, :], 255, None, A.bitwise_and))
+    V(hts, ["hb2"], lambda: v.tensor_scalar(T.hb[0:64, 192:288], T.ht[0:64, :], 1.0, None, A.min))
+    V(["hhi"], ["hb0"], lambda: v.tensor_copy(T.hb[0:64, 0:96], T.hhi[0:64, :]))
+    V(["hlo"], ["hb1"], lambda: v.tensor_copy(T.hb[0:64, 96:192], T.hlo[0:64, :]))
+    tws = []
+    for x in (2, 0, 1):
+        for s in range(4):
+            deps("s", ["tw"], [])
+            dma("s", T.tw[32 * s + x:32 * s + 32:16, :], T.hb[0:64, 96 * x:96 * x + 96], ["hb%d" % x], ["tw%d%d" % (x, s)])
+            tws.append("tw%d%d" % (x, s))
+
+    def spread(q, idx):
+        src, keys = (T.ks, ksk) if q == me else (T.kin, ["kin%d" % q])
+        for half in range(2):
+            k = 4 + 2 * (idx % 2) + half
+            for j in range(2):
+                comp("t", keys + ["r%d" % (2 * half + j)], ["ps%d" % k],
+                     lambda: pe.matmul(ps[k][:, 192 * j:192 * j + 192], T["r%d" % (2 * half + j)][:],
+                                       src[:, 192 * q:192 * q + 192], True, True))
+            for j in range(2):
+                n = 2 * half + j
+                o = T.win[:, M * q + n:M * q + M:4]
+                i = ps[k][:, 192 * j:192 * j + 192]
+                if half == 0:
+                    V(["ps%d" % k], ["w%d%d" % (q, n)], lambda: v.tensor_copy(o, i))
+                else:
+                    act(["ps%d" % k], ["w%d%d" % (q, n)], o, i)
+
+    spread(me, 0)
+
+    V(["lua", "lub", "luc"], ["uh"], lambda: v.tensor_copy(T.uh[0:8, :], T.lu[0:8, :]))
+    third = list(enumerate(((0, 512), (512, 1024), (1024, 1040))))
+    for k, (a, b) in third:
+        comp("t", ["uh", "e8"], ["ps%d" % k],
+             lambda: pe.matmul(ps[k][:, 0:b - a], T.e8[0:8, :], T.uh[0:8, a:b], True, True))
+    calls = []
+    for i in range(16):
+        calls.append(lambda i=i: pe.matmul(ps[3][:, 0:64], T.f8s[0:8, 15 - i:143 - i], T.uh[0:8, i:1024:16], i == 0, False))
+        calls.append(lambda i=i: pe.matmul(ps[3][:, 0:64], T.f8[0:8, 15 - i:143 - i], T.uh[0:8, i + 1:i + 1010:16], False,
+                                           i == 15))
+    comp("t", ["uh", "f8", "f8s"], ["ps3"], calls)
+    for k, (a, b) in third:
+        V(["ps%d" % k, "pcf"], ["em%d" % k],
+          lambda: v.tensor_scalar(T.em[:, a:b], ps[k][:, 0:b - a], T.pcf[:], None, A.is_equal))
+    V(["ps3"], ["ci"], lambda: v.tensor_copy(T.ci[:], ps[3][:, 0:64]))
+    V(["ps3"], ["cu"], lambda: v.tensor_copy(T.cu[:], ps[3][:, 0:64]))
+    V(["ci"], ["oi"], lambda: v.tensor_scalar(T.oi[:], T.ci[:], 6, None, A.arith_shift_right))
+    V(["oi"], ["ownl"], lambda: v.tensor_scalar(T.ownl[:], T.oi[:], float(M), None, A.mult))
+
+    V(["wi", "wj"], ["w1"], lambda: v.tensor_tensor(T.w1[:], T.wj[:], T.wi[:], A.add))
+    for k in (2, 3, 4):
+        V(["wf", "wab"], ["w%d" % k],
+          lambda: v.tensor_scalar(T["w%d" % k][:], T.wf[:], float(k), T.wab[:], A.mult, A.add))
+    for k in (1, 2, 3, 4):
+        V(["ix", "k16", "w%d" % k], ["tw_%d" % k],
+          lambda: v.tensor_scalar(T["tw%d" % k][:], T.ix[:], T.k16[:], T["w%d" % k][:], A.is_equal, A.mult))
+
+    for idx, q in enumerate(others):
+        spread(q, idx + 1)
+
+    wk = ["w%d%d" % (q, n) for q in range(4) for n in range(4)]
+    V(wk, ["n1s"], lambda: v.tensor_reduce(T.n1s[:], T.win[:, 1::M], AxisListType.X, A.add))
+    V(["n1s", "own1"], ["n1u"], lambda: v.tensor_scalar(T.n1u[:, 0:1], T.n1s[:], T.own1[:], None, A.add))
+    V(wk + ["n1u", "own16"], ["n2f"],
+      lambda: v.tensor_tensor(T.n2f[:], T.win[:, 0:3072].indirect(T.n1u[:, 0:1]), T.own16[:], A.add))
+    V(["n2f"], ["n2u"], lambda: v.tensor_copy(T.n2u[:], T.n2f[:]))
+    V(wk + ["n2u"], ["nw"], lambda: v.tensor_copy(T.nw[:], T.win[:, 0:3072].indirect(T.n2u[:, 0:16])))
+
+    act(tws + ["tw", "n1u"], ["g1"], T.g1[:], T.tw[:, 0:3072].indirect(T.n1u[:, 0:1]))
+    act(["g1", "expu"], ["g1e"], T.g1e[:], T.g1[:, 0:16].indirect(T.expu[:, 0:16]))
+    act(tws + ["n2u"], ["g2"], T.g2[:], T.tw[:, 0:3072].indirect(T.n2u[:, 0:16]))
+    comp("t", ["g1e", "g2", "shb", "ib"], ["ps0"],
+         [lambda: pe.matmul(ps[0][:, 0:256], T.shb[:], T.g1e[:], True, False),
+          lambda: pe.matmul(ps[0][:, 0:256], T.ib[:], T.g2[:], False, True)])
+    act(["ps0"], ["g12"], T.g12[:], ps[0][:, 0:256])
+
+    ems = ["em0", "em1", "em2"]
+
+    def nodes(bank, p, out):
+        calls = [lambda: pe.matmul(ps[bank][:, 0:64], T.ih[:], T.ownl[:], True, False)]
+        for i in range(16):
+            calls.append(lambda i=i: pe.matmul(ps[bank][:, 0:64], T.t1h[:, 15 - i:143 - i], T[p][:, i::16], False, i == 15))
+        comp("t", [p, "ownl", "ih", "t1h"], ["ps%d" % bank], calls)
+        V(["ps%d" % bank], [out], lambda: v.tensor_copy(T[out][:], ps[bank][:, 0:64]))
+
+    def value(k, bank, rep, keys, part):
+        calls = []
+        for i in part:
+            calls.append(lambda i=i: pe.matmul(ps[bank][:, 0:64], T["tw%d" % k][:, 15 - i:143 - i],
+                                               T[rep][:, 64 * i:64 * i + 64], i == 0, i == 15))
+        comp("t", keys + ["tw_%d" % k], ["ps%d" % bank], calls)
+
+    V(["nw", "cu"] + ems, ["p3"],
+      lambda: v.tensor_tensor(T.p3[:], T.nw[:, 0:256].indirect(T.cu[:, 0:64]), T.em[:, 2:1026], A.mult))
+    nodes(3, "p3", "n3u")
+    act(["g12", "cu"], ["i12"], T.i12[:], T.g12[:, 0:256].indirect(T.cu[:, 0:64]))
+    V(wk + ["n3u"] + ems, ["p4"],
+      lambda: v.tensor_tensor(T.p4[:], T.win[:, 0:3072].indirect(T.n3u[:, 0:64]), T.em[:, 3:1027], A.mult))
+    act(tws + ["n3u"], ["i3"], T.i3[:], T.tw[:, 0:3072].indirect(T.n3u[:, 0:64]))
+    value(2, 1, "i12", ["i12"], range(16))
+    value(1, 4, "i12", ["i12"], range(8))
+    nodes(2, "p4", "n4u")
+    value(1, 4, "i12", ["i12"], range(8, 16))
+    V(tws + ["n4u"], ["i4a"], lambda: v.tensor_copy(T.i4[:, 0:512], T.tw[:, 0:3072].indirect(T.n4u[:, 0:32])))
+    act(tws + ["n4u"], ["i4b"], T.i4[:, 512:1024], T.tw[:, 0:3072].indirect(T.n4u[:, 32:64]))
+    value(3, 5, "i3", ["i3"], range(16))
+    value(4, 6, "i4", ["i4a"], range(8))
+    value(4, 6, "i4", ["i4b"], range(8, 16))
+    V(["ps4"], ["b1"], lambda: v.tensor_copy(T.b1[:], ps[4][:, 0:64]))
+    V(["ps1", "b1"], ["b2"], lambda: v.tensor_tensor(T.b2[:], ps[1][:, 0:64], T.b1[:], A.max))
+    V(["ps5", "b2"], ["b3"], lambda: v.tensor_tensor(T.b3[:], ps[5][:, 0:64], T.b2[:], A.max))
+    mc = slice(64 * me, 64 * me + 64)
+    V(["ps6", "b3"], ["res%d" % me], lambda: v.tensor_tensor(T.res[:, mc], ps[6][:, 0:64], T.b3[:], A.max))
+
+    deps("g", ["res%d" % me], [])
+    eng = topo.engines(core, cores[others[0]])
+    g.remote_dma_fused([RemoteDMATransfer(dst_ids=[dst(cores[q]) for q in others], dma_engine_mask=bits(eng),
+                                          remote_sem=T.sem["rr%d" % me], srcs=[T.res[:, mc]],
+                                          dsts=[T.res[:, mc] for q in others])], local_sem=T.sem.sr)
+    total["sr"] = len(eng)
+    for q in others:
+        arrive("rr%d" % q, len(topo.engines(cores[q], core)), ["res%d" % q])
+    pr = slice(32 * me, 32 * me + 32)
+    near = [q for q in others if topo.mates(topo.chip(core), topo.chip(cores[q]))]
+    near += [q for q in others if topo.same_plane(topo.chip(core), topo.chip(cores[q]))]
+    for q in [me] + near + [q for q in others if q not in near]:
+        c = slice(64 * q, 64 * q + 64)
+        V(["res%d" % q], ["li%d" % q], lambda: v.tensor_scalar(T.li[pr, c], T.res[pr, c], 16, None, A.arith_shift_right))
+        V(["res%d" % q], ["ii%d" % q], lambda: v.tensor_scalar(T.ii[pr, c], T.res[pr, c], 65535, None, A.bitwise_and))
+        V(["li%d" % q], ["yl%d" % q], lambda: v.tensor_copy(T.yl[pr, c], T.li[pr, c]))
+        V(["ii%d" % q], ["yi%d" % q], lambda: v.tensor_copy(T.yi[pr, c], T.ii[pr, c]))
+        dma("s", T.ylen[2 * q:2 * q + 2, :], T.yl[pr, c], ["yl%d" % q], ["ol%d" % q])
+        dma("a", T.yid[2 * q:2 * q + 2, :], T.yi[pr, c], ["yi%d" % q], ["oi%d" % q])
+
+    for s in total:
+        if seen.get(s, 0) < total[s]:
+            wait("g", [(s, total[s])])

@@ -4,6 +4,7 @@ from concourse.mybir import AluOpType as A, AxisListType, ActivationFunctionType
 
 NR = 4
 M = 768
+RND = 12582912.0
 HF = "float16"
 BF = "bfloat16"
 F32 = "float32"
@@ -19,16 +20,16 @@ SCRATCH = {
     "lbuf": ("dram", [4, 128, 16], I32), "lin": ("dram", [4, 128, 16], I32),
     "tbuf": ("dram", [4, 128, 12], I32), "tin": ("dram", [4, 128, 12], I32),
     "kx": sb([12, 64], I32), "kh": sb([6, 128], HF), "ks": sb(768, HF), "kin": sb(768, HF),
-    "win": sb(3072, F32), "tw": sb(3072, BF), "nw": sb(256, F32),
+    "win": sb(3072, F32), "tw": sb(3072, BF), "nw": sb(256, F32), "nh": sb(64, BF),
     "ht": sb(96, I32), "hhi": sb(96, I32), "hlo": sb(96, I32), "hb": sb(288, BF),
-    "lu": sb(1040, I32), "uh": sb(1040, BF), "em": sb(1040, BF),
+    "lu": sb(1040, I32), "uh": sb(1040, BF), "ea": sb(512, BF), "em": sb(1040, BF),
     "pi": sb(1, I32), "pci": sb(1, I32), "pgi": sb(1, I32), "poi": sb(1, I32),
-    "kf": sb(1, F32), "pcf": sb(1, F32), "k16": sb(1, F32), "own1": sb(1, F32), "k168": sb(1, F32),
+    "kf": sb(1, F32), "pcf": sb(1, F32), "npc": sb(1, F32), "k16": sb(1, F32), "own1": sb(1, F32), "k168": sb(1, F32),
     "imk": sb(128, F32), "ix": sb(143, F32), "mi": sb(128, I32), "own16": sb(16, F32), "expi": sb(16, I32),
     "expu": sb(16, U16), "ma": sb(128, I32), "mb": sb(128, I32), "mc": sb(128, F32), "fm": sb(128, F32),
     "pm": sb(128, I32), "e8": sb(128, BF), "f8": sb(143, BF), "f8s": sb(143, BF),
     "r0": sb(128, HF), "r1": sb(128, HF), "r2": sb(128, HF), "r3": sb(128, HF),
-    "ih": sb(128, HF), "ib": sb(128, BF), "shb": sb(128, BF), "t1h": sb(143, HF),
+    "ih": sb(128, HF), "ib": sb(128, BF), "shb": sb(128, BF), "t1h": sb(143, HF), "t1b": sb(143, BF),
     "wa": sb(1, F32), "wb": sb(1, F32), "wab": sb(1, F32), "wf": sb(1, F32), "wg": sb(1, F32), "wh": sb(1, F32),
     "wi": sb(1, F32), "wj": sb(1, F32),
     "w1": sb(1, F32), "w2": sb(1, F32), "w3": sb(1, F32), "w4": sb(1, F32),
@@ -39,7 +40,7 @@ SCRATCH = {
     "g1": sb(16, BF), "g1e": sb(256, BF), "g2": sb(256, BF), "g12": sb(256, BF),
     "i12": sb(1024, BF), "i3": sb(1024, BF), "i4": sb(1024, BF),
     "b1": sb(64, F32), "b2": sb(64, F32), "b3": sb(64, F32),
-    "res": sb(256, I32), "li": sb(256, I32), "ii": sb(256, I32), "yl": sb(256, F32), "yi": sb(256, F32),
+    "res": sb(256, F32), "rt": sb(256, F32), "yl": sb(256, F32), "yi": sb(256, F32),
 }
 for _i in range(8):
     SCRATCH["ps%d" % _i] = ("psum", [128, 512], F32)
@@ -71,6 +72,9 @@ def rank_program(g, core, T, topo):
         return
     cores = list(T.cores)
     others = [q for q in range(NR) if q != me]
+    near = [q for q in others if topo.mates(topo.chip(core), topo.chip(cores[q]))]
+    near += [q for q in others if topo.same_plane(topo.chip(core), topo.chip(cores[q]))]
+    near += [q for q in others if q not in near]
     q_of = {"g": g, "v": g.vector, "a": g.scalar, "t": g.tensor, "s": g.sync}
     csem = {"g": "cg", "v": "cv", "a": "ca", "t": "ct"}
     total = {}
@@ -173,33 +177,38 @@ def rank_program(g, core, T, topo):
         arrive("rl%d" % q, got(q), ["lin%d" % q])
         arrive("rt%d" % q, got(q), ["tin%d" % q])
 
-    V(["imk"], ["ih"], lambda: v.tensor_scalar(T.ih[:], T.imk[:], 0.0, None, A.is_equal))
+    comp("a", ["imk"], ["tz0"], lambda: g.scalar.activation(T.tw[:, 0:128], T.imk[:], F.Copy, scale=0.0))
+    tz = ["tz0"]
+    for a, b in ((128, 256), (256, 512), (512, 1024), (1024, 2048), (2048, 3072)):
+        act(list(tz), ["tz%d" % a], T.tw[:, a:b], T.tw[:, 0:b - a])
+        tz.append("tz%d" % a)
+
+    V([], ["nh"], lambda: v.memset(T.nh[:], -0.5))
     V(["pi"], ["pci"], lambda: v.tensor_scalar(T.pci[:], T.pi[:], 15, None, A.bitwise_and))
     V(["pi"], ["pgi"], lambda: v.tensor_scalar(T.pgi[:], T.pi[:], 112, None, A.bitwise_and))
     V(["pi"], ["poi"], lambda: v.tensor_scalar(T.poi[:], T.pi[:], 12, None, A.bitwise_and))
     V(["pi"], ["kf"], lambda: v.tensor_copy(T.kf[:], T.pi[:]))
+    V(["pci"], ["pcf"], lambda: v.tensor_copy(T.pcf[:], T.pci[:]))
+    V(["imk"], ["ih"], lambda: v.tensor_scalar(T.ih[:], T.imk[:], 0.0, None, A.is_equal))
     V(["mi"], ["ma"], lambda: v.tensor_scalar(T.ma[:], T.mi[:], 15, None, A.bitwise_and))
     V(["mi"], ["mb"], lambda: v.tensor_scalar(T.mb[:], T.mi[:], 16, None, A.bitwise_and))
-    V(["mi"], ["pm"], lambda: v.tensor_scalar(T.pm[0:8, :], T.mi[0:8, :], 4, None, A.arith_shift_right))
-    V(["pci"], ["pcf"], lambda: v.tensor_copy(T.pcf[:], T.pci[:]))
     V(["pgi"], ["k16"], lambda: v.tensor_scalar(T.k16[:], T.pgi[:], 15.0, None, A.add))
     V(["poi"], ["own1"], lambda: v.tensor_scalar(T.own1[:], T.poi[:], 192.0, None, A.mult))
-    V(["kf"], ["k168"], lambda: v.tensor_scalar(T.k168[0:8, :], T.kf[0:8, :], 16.0, 15.0, A.mult, A.add))
     V(["mb"], ["mc"], lambda: v.tensor_scalar(T.mc[:], T.mb[:], 4.0, None, A.mult))
-    V(["pm", "kf"], ["e8"], lambda: v.tensor_scalar(T.e8[0:8, :], T.pm[0:8, :], T.kf[0:8, :], None, A.is_equal))
+    V(["pcf"], ["npc"], lambda: v.tensor_scalar(T.npc[:], T.pcf[:], -1.0, None, A.mult))
     V(["mc", "ma"], ["fm"], lambda: v.tensor_tensor(T.fm[:], T.mc[:], T.ma[:], A.add))
-    V(["ix", "k168"], ["f8"], lambda: v.tensor_scalar(T.f8[0:8, :], T.ix[0:8, :], T.k168[0:8, :], None, A.is_equal))
-    V(["ix", "k168"], ["f8s"],
-      lambda: v.tensor_scalar(T.f8s[0:8, :], T.ix[0:8, :], T.k168[0:8, :], 16.0, A.is_equal, A.mult))
+    V(["kf"], ["k168"], lambda: v.tensor_scalar(T.k168[0:8, :], T.kf[0:8, :], 16.0, 15.0, A.mult, A.add))
     for n in range(4):
         V(["fm", "kf"], ["r%d" % n],
           lambda: v.tensor_scalar(T["r%d" % n][:], T.fm[:], T.kf[:], float(-16 * n), A.subtract, A.is_equal))
 
-    for la in range(2):
-        V(["kx%d" % la], ["kh%d" % la],
-          lambda: v.tensor_copy(T.kh[:, :, 64 * la:64 * la + 64], T.kx[:, 6 * la:6 * la + 6, :]))
+    for hf in range(2):
+        for la in range(2):
+            V(["kx%d" % la], ["kh%d%d" % (la, hf)],
+              lambda: v.tensor_copy(T.kh[:, 3 * hf:3 * hf + 3, 64 * la:64 * la + 64],
+                                    T.kx[:, 6 * la + 3 * hf:6 * la + 3 * hf + 3, :]))
     for b in range(6):
-        comp("t", ["kh0", "kh1", "ih"], ["ps%d" % (b // 2)],
+        comp("t", ["kh0%d" % (b // 3), "kh1%d" % (b // 3), "ih"], ["ps%d" % (b // 2)],
              lambda: pe.matmul(ps[b // 2][:, 128 * (b % 2):128 * (b % 2) + 128], T.kh[:, b, :], T.ih[:], True, True))
     for b in range(6):
         V(["ps%d" % (b // 2)], ["ks%d" % b],
@@ -217,29 +226,11 @@ def rank_program(g, core, T, topo):
     for la in range(2):
         dma("s", T.ht[32 * la:32 * la + 32, :], T.tin[:, 64 * la:64 * la + 64, :], tins, ["ht%d" % la])
 
-    V([], ["tw"], lambda: v.memset(T.tw[:], 0.0))
-    V(["ix", "k16"], ["t1h"], lambda: v.tensor_scalar(T.t1h[:], T.ix[:], T.k16[:], None, A.is_equal))
-    V(["imk"], ["ib"], lambda: v.tensor_scalar(T.ib[:], T.imk[:], 0.0, None, A.is_equal))
-    V(["imk"], ["shb"], lambda: v.tensor_scalar(T.shb[:], T.imk[:], 3.0, None, A.is_equal))
-    V(["expi"], ["expu"], lambda: v.tensor_copy(T.expu[:], T.expi[:]))
-    for nm, c, wt in (("wa", 0, 256.0), ("wb", 1, 1.0), ("wf", 2, 65536.0), ("wg", 3, 256.0), ("wh", 4, 1.0),
-                      ("wi", 5, 65536.0)):
-        V(["pcf"], [nm], lambda: v.tensor_scalar(T[nm][:], T.pcf[:], float(c), wt, A.is_equal, A.mult))
-    V(["wa", "wb"], ["wab"], lambda: v.tensor_tensor(T.wab[:], T.wa[:], T.wb[:], A.add))
-    V(["wg", "wh"], ["wj"], lambda: v.tensor_tensor(T.wj[:], T.wg[:], T.wh[:], A.add))
-
-    hts = ["ht0", "ht1"]
-    V(hts, ["hhi"], lambda: v.tensor_scalar(T.hhi[0:64, :], T.ht[0:64, :], 8, None, A.arith_shift_right))
-    V(hts, ["hlo"], lambda: v.tensor_scalar(T.hlo[0:64, :], T.ht[0:64, :], 255, None, A.bitwise_and))
-    V(hts, ["hb2"], lambda: v.tensor_scalar(T.hb[0:64, 192:288], T.ht[0:64, :], 1.0, None, A.min))
-    V(["hhi"], ["hb0"], lambda: v.tensor_copy(T.hb[0:64, 0:96], T.hhi[0:64, :]))
-    V(["hlo"], ["hb1"], lambda: v.tensor_copy(T.hb[0:64, 96:192], T.hlo[0:64, :]))
-    tws = []
-    for x in (2, 0, 1):
-        for s in range(4):
-            deps("s", ["tw"], [])
-            dma("s", T.tw[32 * s + x:32 * s + 32:16, :], T.hb[0:64, 96 * x:96 * x + 96], ["hb%d" % x], ["tw%d%d" % (x, s)])
-            tws.append("tw%d%d" % (x, s))
+    V(["mi"], ["pm"], lambda: v.tensor_scalar(T.pm[0:8, :], T.mi[0:8, :], 4, None, A.arith_shift_right))
+    V(["ix", "k168"], ["f8"], lambda: v.tensor_scalar(T.f8[0:8, :], T.ix[0:8, :], T.k168[0:8, :], None, A.is_equal))
+    V(["ix", "k168"], ["f8s"],
+      lambda: v.tensor_scalar(T.f8s[0:8, :], T.ix[0:8, :], T.k168[0:8, :], 16.0, A.is_equal, A.mult))
+    V(["pm", "kf"], ["e8"], lambda: v.tensor_scalar(T.e8[0:8, :], T.pm[0:8, :], T.kf[0:8, :], None, A.is_equal))
 
     def spread(q, idx):
         src, keys = (T.ks, ksk) if q == me else (T.kin, ["kin%d" % q])
@@ -260,35 +251,58 @@ def rank_program(g, core, T, topo):
 
     spread(me, 0)
 
-    V(["lua", "lub", "luc"], ["uh"], lambda: v.tensor_copy(T.uh[0:8, :], T.lu[0:8, :]))
-    third = list(enumerate(((0, 512), (512, 1024), (1024, 1040))))
-    for k, (a, b) in third:
-        comp("t", ["uh", "e8"], ["ps%d" % k],
+    V(["ix", "k16"], ["t1b"], lambda: v.tensor_scalar(T.t1b[:], T.ix[:], T.k16[:], None, A.is_equal))
+    for nm, c, wt in (("wa", 0, 2.0 ** -8), ("wb", 1, 2.0 ** -16), ("wf", 2, 1.0), ("wg", 3, 2.0 ** -8),
+                      ("wh", 4, 2.0 ** -16), ("wi", 5, 1.0)):
+        V(["pcf"], [nm], lambda: v.tensor_scalar(T[nm][:], T.pcf[:], float(c), wt, A.is_equal, A.mult))
+    V(["wa", "wb"], ["wab"], lambda: v.tensor_tensor(T.wab[:], T.wa[:], T.wb[:], A.add))
+    V(["wg", "wh"], ["wj"], lambda: v.tensor_tensor(T.wj[:], T.wg[:], T.wh[:], A.add))
+    for k in (2, 3, 4):
+        V(["wf", "wab"], ["w%d" % k],
+          lambda: v.tensor_scalar(T["w%d" % k][:], T.wf[:], float(k), T.wab[:], A.mult, A.add))
+    V(["wi", "wj"], ["w1"], lambda: v.tensor_tensor(T.w1[:], T.wj[:], T.wi[:], A.add))
+    for k in (2, 3, 4, 1):
+        comp("a", ["t1b", "w%d" % k], ["tw_%d" % k],
+             lambda: g.scalar.activation(T["tw%d" % k][:], T.t1b[:], F.Identity, scale=T["w%d" % k][:]))
+
+    V(["lua"], ["uha"], lambda: v.tensor_copy(T.uh[0:8, 0:512], T.lu[0:8, 0:512]))
+    V(["lua", "lub", "luc"], ["uhb"], lambda: v.tensor_copy(T.uh[0:8, 512:1040], T.lu[0:8, 512:1040]))
+    for k, a, b, uk in ((1, 0, 512, "uha"), (0, 512, 1024, "uhb"), (2, 1024, 1040, "uhb")):
+        comp("t", [uk, "e8"], ["ps%d" % k],
              lambda: pe.matmul(ps[k][:, 0:b - a], T.e8[0:8, :], T.uh[0:8, a:b], True, True))
+    comp("a", ["ps1", "npc"], ["ea"], lambda: g.scalar.activation(T.ea[:], ps[1][:, 0:512], F.Abs, bias=T.npc[:]))
+    comp("a", ["ea"], ["em1"], lambda: g.scalar.activation(T.em[:, 0:512], T.ea[:], F.Relu, bias=1.0, scale=-1.0))
+
+    hts = ["ht0", "ht1"]
+    V(hts, ["hhi"], lambda: v.tensor_scalar(T.hhi[0:64, :], T.ht[0:64, :], 8, None, A.arith_shift_right))
+    V(hts, ["hlo"], lambda: v.tensor_scalar(T.hlo[0:64, :], T.ht[0:64, :], 255, None, A.bitwise_and))
+    V(hts, ["hb2"], lambda: v.tensor_scalar(T.hb[0:64, 192:288], T.ht[0:64, :], 1.0, None, A.min))
+    V(["hhi"], ["hb0"], lambda: v.tensor_copy(T.hb[0:64, 0:96], T.hhi[0:64, :]))
+    V(["hlo"], ["hb1"], lambda: v.tensor_copy(T.hb[0:64, 96:192], T.hlo[0:64, :]))
+    tws = []
+    for x in (2, 0, 1):
+        for s in range(4):
+            deps("s", tz, [])
+            dma("s", T.tw[32 * s + x:32 * s + 32:16, :], T.hb[0:64, 96 * x:96 * x + 96], ["hb%d" % x], ["tw%d%d" % (x, s)])
+            tws.append("tw%d%d" % (x, s))
+    for k, a, b in ((0, 512, 1024), (2, 1024, 1040)):
+        V(["ps%d" % k, "pcf"], ["em%d" % k],
+          lambda: v.tensor_scalar(T.em[:, a:b], ps[k][:, 0:b - a], T.pcf[:], None, A.is_equal))
+    ems = ["em0", "em1", "em2"]
+    V(["imk"], ["ib"], lambda: v.tensor_scalar(T.ib[:], T.imk[:], 0.0, None, A.is_equal))
+    V(["imk"], ["shb"], lambda: v.tensor_scalar(T.shb[:], T.imk[:], 3.0, None, A.is_equal))
+    V(["expi"], ["expu"], lambda: v.tensor_copy(T.expu[:], T.expi[:]))
+    V(["ix", "k16"], ["t1h"], lambda: v.tensor_scalar(T.t1h[:], T.ix[:], T.k16[:], None, A.is_equal))
+
+    for idx, q in enumerate(near):
+        spread(q, idx + 1)
+
     calls = []
     for i in range(16):
         calls.append(lambda i=i: pe.matmul(ps[3][:, 0:64], T.f8s[0:8, 15 - i:143 - i], T.uh[0:8, i:1024:16], i == 0, False))
         calls.append(lambda i=i: pe.matmul(ps[3][:, 0:64], T.f8[0:8, 15 - i:143 - i], T.uh[0:8, i + 1:i + 1010:16], False,
                                            i == 15))
-    comp("t", ["uh", "f8", "f8s"], ["ps3"], calls)
-    for k, (a, b) in third:
-        V(["ps%d" % k, "pcf"], ["em%d" % k],
-          lambda: v.tensor_scalar(T.em[:, a:b], ps[k][:, 0:b - a], T.pcf[:], None, A.is_equal))
-    V(["ps3"], ["ci"], lambda: v.tensor_copy(T.ci[:], ps[3][:, 0:64]))
-    V(["ps3"], ["cu"], lambda: v.tensor_copy(T.cu[:], ps[3][:, 0:64]))
-    V(["ci"], ["oi"], lambda: v.tensor_scalar(T.oi[:], T.ci[:], 6, None, A.arith_shift_right))
-    V(["oi"], ["ownl"], lambda: v.tensor_scalar(T.ownl[:], T.oi[:], float(M), None, A.mult))
-
-    V(["wi", "wj"], ["w1"], lambda: v.tensor_tensor(T.w1[:], T.wj[:], T.wi[:], A.add))
-    for k in (2, 3, 4):
-        V(["wf", "wab"], ["w%d" % k],
-          lambda: v.tensor_scalar(T["w%d" % k][:], T.wf[:], float(k), T.wab[:], A.mult, A.add))
-    for k in (1, 2, 3, 4):
-        V(["ix", "k16", "w%d" % k], ["tw_%d" % k],
-          lambda: v.tensor_scalar(T["tw%d" % k][:], T.ix[:], T.k16[:], T["w%d" % k][:], A.is_equal, A.mult))
-
-    for idx, q in enumerate(others):
-        spread(q, idx + 1)
+    comp("t", ["uha", "uhb", "f8", "f8s"], ["ps3"], calls)
 
     wk = ["w%d%d" % (q, n) for q in range(4) for n in range(4)]
     V(wk, ["n1s"], lambda: v.tensor_reduce(T.n1s[:], T.win[:, 1::M], AxisListType.X, A.add))
@@ -297,8 +311,9 @@ def rank_program(g, core, T, topo):
       lambda: v.tensor_tensor(T.n2f[:], T.win[:, 0:3072].indirect(T.n1u[:, 0:1]), T.own16[:], A.add))
     V(["n2f"], ["n2u"], lambda: v.tensor_copy(T.n2u[:], T.n2f[:]))
     V(wk + ["n2u"], ["nw"], lambda: v.tensor_copy(T.nw[:], T.win[:, 0:3072].indirect(T.n2u[:, 0:16])))
+    V(["ps3"], ["cu"], lambda: v.tensor_copy(T.cu[:], ps[3][:, 0:64]))
 
-    act(tws + ["tw", "n1u"], ["g1"], T.g1[:], T.tw[:, 0:3072].indirect(T.n1u[:, 0:1]))
+    act(tws + ["n1u"], ["g1"], T.g1[:], T.tw[:, 0:3072].indirect(T.n1u[:, 0:1]))
     act(["g1", "expu"], ["g1e"], T.g1e[:], T.g1[:, 0:16].indirect(T.expu[:, 0:16]))
     act(tws + ["n2u"], ["g2"], T.g2[:], T.tw[:, 0:3072].indirect(T.n2u[:, 0:16]))
     comp("t", ["g1e", "g2", "shb", "ib"], ["ps0"],
@@ -306,40 +321,53 @@ def rank_program(g, core, T, topo):
           lambda: pe.matmul(ps[0][:, 0:256], T.ib[:], T.g2[:], False, True)])
     act(["ps0"], ["g12"], T.g12[:], ps[0][:, 0:256])
 
-    ems = ["em0", "em1", "em2"]
-
-    def nodes(bank, p, out):
-        calls = [lambda: pe.matmul(ps[bank][:, 0:64], T.ih[:], T.ownl[:], True, False)]
-        for i in range(16):
-            calls.append(lambda i=i: pe.matmul(ps[bank][:, 0:64], T.t1h[:, 15 - i:143 - i], T[p][:, i::16], False, i == 15))
-        comp("t", [p, "ownl", "ih", "t1h"], ["ps%d" % bank], calls)
-        V(["ps%d" % bank], [out], lambda: v.tensor_copy(T[out][:], ps[bank][:, 0:64]))
-
-    def value(k, bank, rep, keys, part):
+    def nodes(bank, p):
         calls = []
-        for i in part:
+        for i in range(16):
+            calls.append(lambda i=i: pe.matmul(ps[bank][:, 0:64], T.t1h[:, 15 - i:143 - i], T[p][:, i::16], i == 0, False))
+        comp("t", [p, "t1h"], ["ps%d" % bank], calls)
+        comp("t", ["ownl", "ih"], ["ps%d" % bank], lambda: pe.matmul(ps[bank][:, 0:64], T.ih[:], T.ownl[:], False, True))
+
+    def value(k, bank, rep, keys, lo, hi, first, last):
+        if first:
+            comp("t", ["nh", "ib"], ["ps%d" % bank], lambda: pe.matmul(ps[bank][:, 0:64], T.ib[:], T.nh[:], True, False))
+        calls = []
+        for i in range(lo, hi):
             calls.append(lambda i=i: pe.matmul(ps[bank][:, 0:64], T["tw%d" % k][:, 15 - i:143 - i],
-                                               T[rep][:, 64 * i:64 * i + 64], i == 0, i == 15))
+                                               T[rep][:, 64 * i:64 * i + 64], False, last and i == hi - 1))
         comp("t", keys + ["tw_%d" % k], ["ps%d" % bank], calls)
 
     V(["nw", "cu"] + ems, ["p3"],
       lambda: v.tensor_tensor(T.p3[:], T.nw[:, 0:256].indirect(T.cu[:, 0:64]), T.em[:, 2:1026], A.mult))
-    nodes(3, "p3", "n3u")
-    act(["g12", "cu"], ["i12"], T.i12[:], T.g12[:, 0:256].indirect(T.cu[:, 0:64]))
+    V(["ps3"], ["ci"], lambda: v.tensor_copy(T.ci[:], ps[3][:, 0:64]))
+    V(["ci"], ["oi"], lambda: v.tensor_scalar(T.oi[:], T.ci[:], 6, None, A.arith_shift_right))
+    V(["oi"], ["ownl"], lambda: v.tensor_scalar(T.ownl[:], T.oi[:], float(M), None, A.mult))
+    nodes(7, "p3")
+    V(["ps7"], ["n3u"], lambda: v.tensor_copy(T.n3u[:], ps[7][:, 0:64]))
+    act(["g12", "cu"], ["i12a"], T.i12[:, 0:512], T.g12[:, 0:256].indirect(T.cu[:, 0:32]))
+    act(["g12", "cu"], ["i12b"], T.i12[:, 512:1024], T.g12[:, 0:256].indirect(T.cu[:, 32:64]))
     V(wk + ["n3u"] + ems, ["p4"],
       lambda: v.tensor_tensor(T.p4[:], T.win[:, 0:3072].indirect(T.n3u[:, 0:64]), T.em[:, 3:1027], A.mult))
     act(tws + ["n3u"], ["i3"], T.i3[:], T.tw[:, 0:3072].indirect(T.n3u[:, 0:64]))
-    value(2, 1, "i12", ["i12"], range(16))
-    value(1, 4, "i12", ["i12"], range(8))
-    nodes(2, "p4", "n4u")
-    value(1, 4, "i12", ["i12"], range(8, 16))
-    V(tws + ["n4u"], ["i4a"], lambda: v.tensor_copy(T.i4[:, 0:512], T.tw[:, 0:3072].indirect(T.n4u[:, 0:32])))
-    act(tws + ["n4u"], ["i4b"], T.i4[:, 512:1024], T.tw[:, 0:3072].indirect(T.n4u[:, 32:64]))
-    value(3, 5, "i3", ["i3"], range(16))
-    value(4, 6, "i4", ["i4a"], range(8))
-    value(4, 6, "i4", ["i4b"], range(8, 16))
+    for hf in range(2):
+        for k, bank in ((2, 1), (1, 4)):
+            value(k, bank, "i12", ["i12%s" % "ab"[hf]], 8 * hf, 8 * hf + 8, hf == 0, hf == 1)
     V(["ps4"], ["b1"], lambda: v.tensor_copy(T.b1[:], ps[4][:, 0:64]))
     V(["ps1", "b1"], ["b2"], lambda: v.tensor_tensor(T.b2[:], ps[1][:, 0:64], T.b1[:], A.max))
+    nodes(2, "p4")
+    V(["ps2"], ["n4u"], lambda: v.tensor_copy(T.n4u[:], ps[2][:, 0:64]))
+    for x in range(2):
+        for y in range(2):
+            q = 2 * y + x
+            o = T.i4[:, 256 * q:256 * q + 256]
+            i = T.tw[:, 0:3072].indirect(T.n4u[:, 16 * q:16 * q + 16])
+            if y == 0:
+                V(tws + ["n4u"], ["i4%d" % q], lambda: v.tensor_copy(o, i))
+            else:
+                act(tws + ["n4u"], ["i4%d" % q], o, i)
+    value(3, 5, "i3", ["i3"], 0, 16, True, True)
+    for n, q in enumerate((0, 2, 1, 3)):
+        value(4, 6, "i4", ["i4%d" % q], 4 * q, 4 * q + 4, n == 0, n == 3)
     V(["ps5", "b2"], ["b3"], lambda: v.tensor_tensor(T.b3[:], ps[5][:, 0:64], T.b2[:], A.max))
     mc = slice(64 * me, 64 * me + 64)
     V(["ps6", "b3"], ["res%d" % me], lambda: v.tensor_tensor(T.res[:, mc], ps[6][:, 0:64], T.b3[:], A.max))
@@ -353,14 +381,13 @@ def rank_program(g, core, T, topo):
     for q in others:
         arrive("rr%d" % q, len(topo.engines(cores[q], core)), ["res%d" % q])
     pr = slice(32 * me, 32 * me + 32)
-    near = [q for q in others if topo.mates(topo.chip(core), topo.chip(cores[q]))]
-    near += [q for q in others if topo.same_plane(topo.chip(core), topo.chip(cores[q]))]
-    for q in [me] + near + [q for q in others if q not in near]:
+    for q in [me] + near:
         c = slice(64 * q, 64 * q + 64)
-        V(["res%d" % q], ["li%d" % q], lambda: v.tensor_scalar(T.li[pr, c], T.res[pr, c], 16, None, A.arith_shift_right))
-        V(["res%d" % q], ["ii%d" % q], lambda: v.tensor_scalar(T.ii[pr, c], T.res[pr, c], 65535, None, A.bitwise_and))
-        V(["li%d" % q], ["yl%d" % q], lambda: v.tensor_copy(T.yl[pr, c], T.li[pr, c]))
-        V(["ii%d" % q], ["yi%d" % q], lambda: v.tensor_copy(T.yi[pr, c], T.ii[pr, c]))
+        V(["res%d" % q], ["yl%d" % q], lambda: v.tensor_scalar(T.yl[pr, c], T.res[pr, c], RND, RND, A.add, A.subtract))
+        V(["res%d" % q, "yl%d" % q], ["rt%d" % q],
+          lambda: v.tensor_tensor(T.rt[pr, c], T.res[pr, c], T.yl[pr, c], A.subtract))
+        comp("a", ["rt%d" % q], ["yi%d" % q],
+             lambda: g.scalar.activation(T.yi[pr, c], T.rt[pr, c], F.Copy, bias=32768.0, scale=65536.0))
         dma("s", T.ylen[2 * q:2 * q + 2, :], T.yl[pr, c], ["yl%d" % q], ["ol%d" % q])
         dma("a", T.yid[2 * q:2 * q + 2, :], T.yi[pr, c], ["yi%d" % q], ["oi%d" % q])
 

@@ -4,7 +4,8 @@ from concourse.mybir import AluOpType as A, AxisListType, ActivationFunctionType
 
 NR = 4
 M = 768
-RND = 12582912.0
+K17 = 131072.0
+RND = 12582912.0 * K17
 HF = "float16"
 BF = "bfloat16"
 F32 = "float32"
@@ -20,18 +21,17 @@ SCRATCH = {
     "lbuf": ("dram", [4, 128, 16], I32), "lin": ("dram", [4, 128, 16], I32),
     "tbuf": ("dram", [4, 128, 12], I32), "tin": ("dram", [4, 128, 12], I32),
     "kx": sb([12, 64], I32), "kh": sb([6, 128], HF), "ks": sb(768, HF), "kin": sb(768, HF),
-    "win": sb(3072, F32), "tw": sb(3072, BF), "nw": sb(256, F32), "nh": sb(64, BF),
-    "ht": sb(96, I32), "hhi": sb(96, I32), "hlo": sb(96, I32), "hb": sb(288, BF),
+    "win": sb(3072, F32), "tw": sb(3072, BF), "nw": sb(256, F32),
+    "ht": sb(96, I32), "hb": sb(288, BF),
     "lu": sb(1040, I32), "uh": sb(1040, BF), "ea": sb(512, BF), "em": sb(1040, BF),
     "pi": sb(1, I32), "pci": sb(1, I32), "pgi": sb(1, I32), "poi": sb(1, I32),
-    "kf": sb(1, F32), "pcf": sb(1, F32), "npc": sb(1, F32), "k16": sb(1, F32), "own1": sb(1, F32), "k168": sb(1, F32),
-    "imk": sb(128, F32), "ix": sb(143, F32), "mi": sb(128, I32), "own16": sb(16, F32), "expi": sb(16, I32),
-    "expu": sb(16, U16), "ma": sb(128, I32), "mb": sb(128, I32), "mc": sb(128, F32), "fm": sb(128, F32),
-    "pm": sb(128, I32), "e8": sb(128, BF), "f8": sb(143, BF), "f8s": sb(143, BF),
+    "pcf": sb(1, F32), "npc": sb(1, F32), "k16": sb(1, F32), "own1": sb(1, F32),
+    "imk": sb(128, BF), "frk": sb(128, BF), "ix": sb(143, BF), "e8i": sb(128, BF), "f8i": sb(143, BF),
+    "own16": sb(16, F32), "expi": sb(16, I32), "expu": sb(16, U16),
+    "e8": sb(128, BF), "f8": sb(143, BF), "f8s": sb(143, BF),
     "r0": sb(128, HF), "r1": sb(128, HF), "r2": sb(128, HF), "r3": sb(128, HF),
     "ih": sb(128, HF), "ib": sb(128, BF), "shb": sb(128, BF), "t1h": sb(143, HF), "t1b": sb(143, BF),
-    "wa": sb(1, F32), "wb": sb(1, F32), "wab": sb(1, F32), "wf": sb(1, F32), "wg": sb(1, F32), "wh": sb(1, F32),
-    "wi": sb(1, F32), "wj": sb(1, F32),
+    "wab": sb(1, F32), "wf": sb(1, F32), "wg": sb(1, F32), "wh": sb(1, F32),
     "w1": sb(1, F32), "w2": sb(1, F32), "w3": sb(1, F32), "w4": sb(1, F32),
     "tw1": sb(143, BF), "tw2": sb(143, BF), "tw3": sb(143, BF), "tw4": sb(143, BF),
     "ci": sb(64, I32), "cu": sb(64, U16), "oi": sb(64, I32), "ownl": sb(64, HF),
@@ -44,8 +44,8 @@ SCRATCH = {
 }
 for _i in range(8):
     SCRATCH["ps%d" % _i] = ("psum", [128, 512], F32)
-SEMAPHORES = (["cv", "ca", "ct", "cg", "sl", "st", "sk", "sr"] + ["r%s%d" % (x, i) for x in "ltkr" for i in range(NR)]
-              + ["d%d" % i for i in range(48)])
+SEMAPHORES = (["cv", "ca", "ct", "cg", "sl", "st", "sk0", "sk1", "sr"]
+              + ["r%s%d" % (x, i) for x in "ltkr" for i in range(NR)] + ["d%d" % i for i in range(48)])
 
 
 def shares(topo, src, dsts):
@@ -164,18 +164,23 @@ def rank_program(g, core, T, topo):
     dma("s", T.lin[me], T.lett[2 * me:2 * me + 2, :], [], ["lin%d" % me])
     dma("a", T.tin[me], T.tid[2 * me:2 * me + 2, :], [], ["tin%d" % me])
 
+    def iota(key, out, pattern, base, mult):
+        comp("g", [], [key], lambda: g.iota(out, pattern, base, mult, allow_small_or_imprecise_dtypes=True))
+
     comp("g", [], ["pi"], lambda: g.iota(T.pi[:], [[1, 1]], 0, 1))
-    comp("g", [], ["imk"], lambda: g.iota(T.imk[:], [[1, 128]], 0, -1, allow_small_or_imprecise_dtypes=True))
-    comp("g", [], ["mi"], lambda: g.iota(T.mi[:], [[1, 128]], 0, 0))
-    comp("g", [], ["ix"], lambda: g.iota(T.ix[:], [[1, 143]], 0, 0, allow_small_or_imprecise_dtypes=True))
-    comp("g", [], ["own16"], lambda: g.iota(T.own16[:], [[M, 4], [0, 4]], 0, 0, allow_small_or_imprecise_dtypes=True))
-    comp("g", [], ["expi"], lambda: g.iota(T.expi[:], [[1, 16]], 0, 0))
+    iota("imk", T.imk[:], [[1, 128]], 0, -1)
+    iota("frk", T.frk[:], [[0, 4], [64, 2], [1, 16]], 0, -1)
+    iota("ix", T.ix[:], [[1, 143]], 0, 0)
+    iota("e8i", T.e8i[0:8, :], [[1, 8], [0, 16]], 0, -1)
 
     send("l", "sl", lambda q: T.lbuf[q], T.lin[me], ["lbuf"])
     send("t", "st", lambda q: T.tbuf[q], T.tin[me], ["tbuf"])
     for q in others:
         arrive("rl%d" % q, got(q), ["lin%d" % q])
         arrive("rt%d" % q, got(q), ["tin%d" % q])
+    iota("f8i", T.f8i[0:8, :], [[1, 143]], -15, -16)
+    iota("own16", T.own16[:], [[M, 4], [0, 4]], 0, 0)
+    comp("g", [], ["expi"], lambda: g.iota(T.expi[:], [[1, 16]], 0, 0))
 
     comp("a", ["imk"], ["tz0"], lambda: g.scalar.activation(T.tw[:, 0:128], T.imk[:], F.Copy, scale=0.0))
     tz = ["tz0"]
@@ -183,24 +188,23 @@ def rank_program(g, core, T, topo):
         act(list(tz), ["tz%d" % a], T.tw[:, a:b], T.tw[:, 0:b - a])
         tz.append("tz%d" % a)
 
-    V([], ["nh"], lambda: v.memset(T.nh[:], -0.5))
     V(["pi"], ["pci"], lambda: v.tensor_scalar(T.pci[:], T.pi[:], 15, None, A.bitwise_and))
     V(["pi"], ["pgi"], lambda: v.tensor_scalar(T.pgi[:], T.pi[:], 112, None, A.bitwise_and))
     V(["pi"], ["poi"], lambda: v.tensor_scalar(T.poi[:], T.pi[:], 12, None, A.bitwise_and))
-    V(["pi"], ["kf"], lambda: v.tensor_copy(T.kf[:], T.pi[:]))
     V(["pci"], ["pcf"], lambda: v.tensor_copy(T.pcf[:], T.pci[:]))
-    V(["imk"], ["ih"], lambda: v.tensor_scalar(T.ih[:], T.imk[:], 0.0, None, A.is_equal))
-    V(["mi"], ["ma"], lambda: v.tensor_scalar(T.ma[:], T.mi[:], 15, None, A.bitwise_and))
-    V(["mi"], ["mb"], lambda: v.tensor_scalar(T.mb[:], T.mi[:], 16, None, A.bitwise_and))
     V(["pgi"], ["k16"], lambda: v.tensor_scalar(T.k16[:], T.pgi[:], 15.0, None, A.add))
     V(["poi"], ["own1"], lambda: v.tensor_scalar(T.own1[:], T.poi[:], 192.0, None, A.mult))
-    V(["mb"], ["mc"], lambda: v.tensor_scalar(T.mc[:], T.mb[:], 4.0, None, A.mult))
+    V(["imk"], ["ih"], lambda: v.tensor_scalar(T.ih[:], T.imk[:], 0.0, None, A.is_equal))
     V(["pcf"], ["npc"], lambda: v.tensor_scalar(T.npc[:], T.pcf[:], -1.0, None, A.mult))
-    V(["mc", "ma"], ["fm"], lambda: v.tensor_tensor(T.fm[:], T.mc[:], T.ma[:], A.add))
-    V(["kf"], ["k168"], lambda: v.tensor_scalar(T.k168[0:8, :], T.kf[0:8, :], 16.0, 15.0, A.mult, A.add))
+    V(["pcf"], ["wab"], lambda: v.tensor_scalar(T.wab[:], T.pcf[:], 2.0, None, A.is_lt))
+    V(["pcf"], ["wf"], lambda: v.tensor_scalar(T.wf[:], T.pcf[:], 2.0, K17, A.is_equal, A.mult))
+    V(["imk"], ["ib"], lambda: v.tensor_scalar(T.ib[:], T.imk[:], 0.0, None, A.is_equal))
+    V(["imk"], ["shb"], lambda: v.tensor_scalar(T.shb[:], T.imk[:], 3.0, None, A.is_equal))
     for n in range(4):
-        V(["fm", "kf"], ["r%d" % n],
-          lambda: v.tensor_scalar(T["r%d" % n][:], T.fm[:], T.kf[:], float(-16 * n), A.subtract, A.is_equal))
+        V(["frk"], ["r%d" % n], lambda: v.tensor_scalar(T["r%d" % n][:], T.frk[:], float(-16 * n), None, A.is_equal))
+    for nm in ("t1b", "t1h"):
+        V(["ix", "k16"], [nm], lambda: v.tensor_scalar(T[nm][:], T.ix[:], T.k16[:], None, A.is_equal))
+    V(["e8i"], ["e8"], lambda: v.tensor_scalar(T.e8[0:8, :], T.e8i[0:8, :], 0.0, None, A.is_equal))
 
     for hf in range(2):
         for la in range(2):
@@ -214,9 +218,16 @@ def rank_program(g, core, T, topo):
         V(["ps%d" % (b // 2)], ["ks%d" % b],
           lambda: v.tensor_copy(T.ks[:, b::6], ps[b // 2][:, 128 * (b % 2):128 * (b % 2) + 128]))
     ksk = ["ks%d" % b for b in range(6)]
-    send("k", "sk", lambda q: T.ks[:, 192 * q:192 * q + 192], T.kin[:, 192 * me:192 * me + 192], ksk)
+    eng = topo.engines(core, cores[near[0]])
+    ways = ([(near[0], eng[:len(eng) // 2]), (near[1], eng[len(eng) // 2:])], [(near[2], eng)])
+    deps("g", ksk, [])
+    for n, way in enumerate(ways):
+        g.remote_dma_fused([RemoteDMATransfer(dst_ids=[dst(cores[q])], dma_engine_mask=bits(e), remote_sem=T.sem["rk%d" % me],
+                                              src=T.ks[:, 192 * q:192 * q + 192], dst=T.kin[:, 192 * me:192 * me + 192])
+                            for q, e in way], local_sem=T.sem["sk%d" % n])
+        total["sk%d" % n] = len(eng)
     for q in others:
-        arrive("rk%d" % q, got(q), ["kin%d" % q])
+        arrive("rk%d" % q, len(eng) if q == near[2] else len(eng) // 2, ["kin%d" % q])
 
     lins = ["lin%d" % q for q in range(4)]
     tins = ["tin%d" % q for q in range(4)]
@@ -226,16 +237,13 @@ def rank_program(g, core, T, topo):
     for la in range(2):
         dma("s", T.ht[32 * la:32 * la + 32, :], T.tin[:, 64 * la:64 * la + 64, :], tins, ["ht%d" % la])
 
-    V(["mi"], ["pm"], lambda: v.tensor_scalar(T.pm[0:8, :], T.mi[0:8, :], 4, None, A.arith_shift_right))
-    V(["ix", "k168"], ["f8"], lambda: v.tensor_scalar(T.f8[0:8, :], T.ix[0:8, :], T.k168[0:8, :], None, A.is_equal))
-    V(["ix", "k168"], ["f8s"],
-      lambda: v.tensor_scalar(T.f8s[0:8, :], T.ix[0:8, :], T.k168[0:8, :], 16.0, A.is_equal, A.mult))
-    V(["pm", "kf"], ["e8"], lambda: v.tensor_scalar(T.e8[0:8, :], T.pm[0:8, :], T.kf[0:8, :], None, A.is_equal))
+    V(["f8i"], ["f8"], lambda: v.tensor_scalar(T.f8[0:8, :], T.f8i[0:8, :], 0.0, None, A.is_equal))
+    V(["f8i"], ["f8s"], lambda: v.tensor_scalar(T.f8s[0:8, :], T.f8i[0:8, :], 0.0, 16.0, A.is_equal, A.mult))
 
-    def spread(q, idx):
+    def spread(q, bank):
         src, keys = (T.ks, ksk) if q == me else (T.kin, ["kin%d" % q])
         for half in range(2):
-            k = 4 + 2 * (idx % 2) + half
+            k = bank + half
             for j in range(2):
                 comp("t", keys + ["r%d" % (2 * half + j)], ["ps%d" % k],
                      lambda: pe.matmul(ps[k][:, 192 * j:192 * j + 192], T["r%d" % (2 * half + j)][:],
@@ -249,21 +257,18 @@ def rank_program(g, core, T, topo):
                 else:
                     act(["ps%d" % k], ["w%d%d" % (q, n)], o, i)
 
-    spread(me, 0)
+    spread(me, 4)
 
-    V(["ix", "k16"], ["t1b"], lambda: v.tensor_scalar(T.t1b[:], T.ix[:], T.k16[:], None, A.is_equal))
-    for nm, c, wt in (("wa", 0, 2.0 ** -8), ("wb", 1, 2.0 ** -16), ("wf", 2, 1.0), ("wg", 3, 2.0 ** -8),
-                      ("wh", 4, 2.0 ** -16), ("wi", 5, 1.0)):
-        V(["pcf"], [nm], lambda: v.tensor_scalar(T[nm][:], T.pcf[:], float(c), wt, A.is_equal, A.mult))
-    V(["wa", "wb"], ["wab"], lambda: v.tensor_tensor(T.wab[:], T.wa[:], T.wb[:], A.add))
-    V(["wg", "wh"], ["wj"], lambda: v.tensor_tensor(T.wj[:], T.wg[:], T.wh[:], A.add))
     for k in (2, 3, 4):
         V(["wf", "wab"], ["w%d" % k],
           lambda: v.tensor_scalar(T["w%d" % k][:], T.wf[:], float(k), T.wab[:], A.mult, A.add))
-    V(["wi", "wj"], ["w1"], lambda: v.tensor_tensor(T.w1[:], T.wj[:], T.wi[:], A.add))
+    V(["pcf"], ["wg"], lambda: v.tensor_scalar(T.wg[:], T.pcf[:], 3.0, None, A.is_ge))
+    V(["pcf"], ["wh"], lambda: v.tensor_scalar(T.wh[:], T.pcf[:], 5.0, K17 - 1.0, A.is_ge, A.mult))
+    V(["wg", "wh"], ["w1"], lambda: v.tensor_tensor(T.w1[:], T.wg[:], T.wh[:], A.add))
     for k in (2, 3, 4, 1):
         comp("a", ["t1b", "w%d" % k], ["tw_%d" % k],
              lambda: g.scalar.activation(T["tw%d" % k][:], T.t1b[:], F.Identity, scale=T["w%d" % k][:]))
+    V(["expi"], ["expu"], lambda: v.tensor_copy(T.expu[:], T.expi[:]))
 
     V(["lua"], ["uha"], lambda: v.tensor_copy(T.uh[0:8, 0:512], T.lu[0:8, 0:512]))
     V(["lua", "lub", "luc"], ["uhb"], lambda: v.tensor_copy(T.uh[0:8, 512:1040], T.lu[0:8, 512:1040]))
@@ -274,13 +279,11 @@ def rank_program(g, core, T, topo):
     comp("a", ["ea"], ["em1"], lambda: g.scalar.activation(T.em[:, 0:512], T.ea[:], F.Relu, bias=1.0, scale=-1.0))
 
     hts = ["ht0", "ht1"]
-    V(hts, ["hhi"], lambda: v.tensor_scalar(T.hhi[0:64, :], T.ht[0:64, :], 8, None, A.arith_shift_right))
-    V(hts, ["hlo"], lambda: v.tensor_scalar(T.hlo[0:64, :], T.ht[0:64, :], 255, None, A.bitwise_and))
+    V(hts, ["hb0"], lambda: v.tensor_copy(T.hb[0:64, 0:96], T.ht[0:64, :]))
     V(hts, ["hb2"], lambda: v.tensor_scalar(T.hb[0:64, 192:288], T.ht[0:64, :], 1.0, None, A.min))
-    V(["hhi"], ["hb0"], lambda: v.tensor_copy(T.hb[0:64, 0:96], T.hhi[0:64, :]))
-    V(["hlo"], ["hb1"], lambda: v.tensor_copy(T.hb[0:64, 96:192], T.hlo[0:64, :]))
+    V(hts + ["hb0"], ["hb1"], lambda: v.tensor_tensor(T.hb[0:64, 96:192], T.ht[0:64, :], T.hb[0:64, 0:96], A.subtract))
     tws = []
-    for x in (2, 0, 1):
+    for x in (0, 2, 1):
         for s in range(4):
             deps("s", tz, [])
             dma("s", T.tw[32 * s + x:32 * s + 32:16, :], T.hb[0:64, 96 * x:96 * x + 96], ["hb%d" % x], ["tw%d%d" % (x, s)])
@@ -289,14 +292,9 @@ def rank_program(g, core, T, topo):
         V(["ps%d" % k, "pcf"], ["em%d" % k],
           lambda: v.tensor_scalar(T.em[:, a:b], ps[k][:, 0:b - a], T.pcf[:], None, A.is_equal))
     ems = ["em0", "em1", "em2"]
-    V(["imk"], ["ib"], lambda: v.tensor_scalar(T.ib[:], T.imk[:], 0.0, None, A.is_equal))
-    V(["imk"], ["shb"], lambda: v.tensor_scalar(T.shb[:], T.imk[:], 3.0, None, A.is_equal))
-    V(["expi"], ["expu"], lambda: v.tensor_copy(T.expu[:], T.expi[:]))
-    V(["ix", "k16"], ["t1h"], lambda: v.tensor_scalar(T.t1h[:], T.ix[:], T.k16[:], None, A.is_equal))
 
-    for idx, q in enumerate(near):
-        spread(q, idx + 1)
-
+    for q, bank in zip(near, (6, 4, 1)):
+        spread(q, bank)
     calls = []
     for i in range(16):
         calls.append(lambda i=i: pe.matmul(ps[3][:, 0:64], T.f8s[0:8, 15 - i:143 - i], T.uh[0:8, i:1024:16], i == 0, False))
@@ -329,12 +327,10 @@ def rank_program(g, core, T, topo):
         comp("t", ["ownl", "ih"], ["ps%d" % bank], lambda: pe.matmul(ps[bank][:, 0:64], T.ih[:], T.ownl[:], False, True))
 
     def value(k, bank, rep, keys, lo, hi, first, last):
-        if first:
-            comp("t", ["nh", "ib"], ["ps%d" % bank], lambda: pe.matmul(ps[bank][:, 0:64], T.ib[:], T.nh[:], True, False))
         calls = []
         for i in range(lo, hi):
             calls.append(lambda i=i: pe.matmul(ps[bank][:, 0:64], T["tw%d" % k][:, 15 - i:143 - i],
-                                               T[rep][:, 64 * i:64 * i + 64], False, last and i == hi - 1))
+                                               T[rep][:, 64 * i:64 * i + 64], first and i == lo, last and i == hi - 1))
         comp("t", keys + ["tw_%d" % k], ["ps%d" % bank], calls)
 
     V(["nw", "cu"] + ems, ["p3"],
@@ -373,7 +369,6 @@ def rank_program(g, core, T, topo):
     V(["ps6", "b3"], ["res%d" % me], lambda: v.tensor_tensor(T.res[:, mc], ps[6][:, 0:64], T.b3[:], A.max))
 
     deps("g", ["res%d" % me], [])
-    eng = topo.engines(core, cores[others[0]])
     g.remote_dma_fused([RemoteDMATransfer(dst_ids=[dst(cores[q]) for q in others], dma_engine_mask=bits(eng),
                                           remote_sem=T.sem["rr%d" % me], srcs=[T.res[:, mc]],
                                           dsts=[T.res[:, mc] for q in others])], local_sem=T.sem.sr)
@@ -383,13 +378,12 @@ def rank_program(g, core, T, topo):
     pr = slice(32 * me, 32 * me + 32)
     for q in [me] + near:
         c = slice(64 * q, 64 * q + 64)
-        V(["res%d" % q], ["yl%d" % q], lambda: v.tensor_scalar(T.yl[pr, c], T.res[pr, c], RND, RND, A.add, A.subtract))
-        V(["res%d" % q, "yl%d" % q], ["rt%d" % q],
-          lambda: v.tensor_tensor(T.rt[pr, c], T.res[pr, c], T.yl[pr, c], A.subtract))
-        comp("a", ["rt%d" % q], ["yi%d" % q],
-             lambda: g.scalar.activation(T.yi[pr, c], T.rt[pr, c], F.Copy, bias=32768.0, scale=65536.0))
-        dma("s", T.ylen[2 * q:2 * q + 2, :], T.yl[pr, c], ["yl%d" % q], ["ol%d" % q])
-        dma("a", T.yid[2 * q:2 * q + 2, :], T.yi[pr, c], ["yi%d" % q], ["oi%d" % q])
+        V(["res%d" % q], ["rt%d" % q], lambda: v.tensor_scalar(T.rt[pr, c], T.res[pr, c], RND, RND, A.add, A.subtract))
+        V(["res%d" % q, "rt%d" % q], ["yi%d" % q],
+          lambda: v.tensor_tensor(T.yi[pr, c], T.res[pr, c], T.rt[pr, c], A.subtract))
+        comp("a", ["rt%d" % q], ["yl%d" % q], lambda: g.scalar.activation(T.yl[pr, c], T.rt[pr, c], F.Copy, scale=1.0 / K17))
+        dma("s", T.yid[2 * q:2 * q + 2, :], T.yi[pr, c], ["yi%d" % q], ["oi%d" % q])
+        dma("a", T.ylen[2 * q:2 * q + 2, :], T.yl[pr, c], ["yl%d" % q], ["ol%d" % q])
 
     for s in total:
         if seen.get(s, 0) < total[s]:

@@ -4,6 +4,9 @@ from concourse.mybir import AluOpType as A, AxisListType, ActivationFunctionType
 
 NR = 4
 M = 768
+OFF = 1536.0
+SA, SB = 448, 384
+CUT = 480
 K17 = 131072.0
 RND = 12582912.0 * K17
 HF = "float16"
@@ -23,24 +26,22 @@ SCRATCH = {
     "kx": sb([12, 64], I32), "kh": sb([6, 128], HF), "ks": sb(768, HF), "kin": sb(768, HF),
     "win": sb(3072, F32), "tw": sb(3072, BF), "nw": sb(256, F32),
     "ht": sb(96, I32), "hb": sb(288, BF),
-    "lu": sb(1040, I32), "uh": sb(1040, BF), "ea": sb(512, BF), "em": sb(1040, BF),
-    "pi": sb(1, I32), "pci": sb(1, I32), "pgi": sb(1, I32), "poi": sb(1, I32),
-    "pcf": sb(1, F32), "npc": sb(1, F32), "k16": sb(1, F32), "own1": sb(1, F32),
-    "imk": sb(128, BF), "frk": sb(128, BF), "ix": sb(143, BF), "e8i": sb(128, BF), "f8i": sb(143, BF),
-    "own16": sb(16, F32), "expi": sb(16, I32), "expu": sb(16, U16),
+    "li": sb(1040, I32), "lu": sb(1040, BF), "em": sb(1040, BF),
+    "pi": sb(1, I32), "pci": sb(1, I32), "poi": sb(1, I32),
+    "pcf": sb(1, F32), "k16": sb(1, F32), "own1": sb(1, F32), "f1": sb(1, F32),
+    "imk": sb(143, BF), "frk": sb(128, BF), "e8i": sb(128, BF), "one": sb(128, BF), "kk": sb(3, F32),
+    "expi": sb(16, I32), "expu": sb(16, U16),
     "e8": sb(128, BF), "f8": sb(143, BF), "f8s": sb(143, BF),
     "r0": sb(128, HF), "r1": sb(128, HF), "r2": sb(128, HF), "r3": sb(128, HF),
-    "ih": sb(128, HF), "ib": sb(128, BF), "shb": sb(128, BF), "t1h": sb(143, HF), "t1b": sb(143, BF),
-    "wab": sb(1, F32), "wf": sb(1, F32), "wg": sb(1, F32), "wh": sb(1, F32),
-    "w1": sb(1, F32), "w2": sb(1, F32), "w3": sb(1, F32), "w4": sb(1, F32),
-    "tw1": sb(143, BF), "tw2": sb(143, BF), "tw3": sb(143, BF), "tw4": sb(143, BF),
-    "ci": sb(64, I32), "cu": sb(64, U16), "oi": sb(64, I32), "ownl": sb(64, HF),
-    "n1s": sb(1, F32), "n1u": sb(2, U16), "n2f": sb(16, F32), "n2u": sb(16, U16), "n3u": sb(64, U16), "n4u": sb(64, U16),
+    "ih": sb(128, HF), "id": sb(128, F32), "ib": sb(128, BF), "shb": sb(128, BF), "t1h": sb(143, HF),
+    "wab": sb(1, F32), "wf": sb(1, F32), "wg": sb(1, F32), "wh": sb(1, F32), "w1": sb(1, F32), "wk": sb(3, F32),
+    "vt": sb(32, BF),
+    "cu": sb(64, U16), "n1s": sb(1, F32), "n1u": sb(2, U16), "n2u": sb(16, U16), "n3u": sb(64, U16), "n4u": sb(64, U16),
     "p3": sb(1024, HF), "p4": sb(1024, HF),
     "g1": sb(16, BF), "g1e": sb(256, BF), "g2": sb(256, BF), "g12": sb(256, BF),
     "i12": sb(1024, BF), "i3": sb(1024, BF), "i4": sb(1024, BF),
     "b1": sb(64, F32), "b2": sb(64, F32), "b3": sb(64, F32),
-    "res": sb(256, F32), "rt": sb(256, F32), "yl": sb(256, F32), "yi": sb(256, F32),
+    "res": sb(64, F32), "rcv": sb(64, F32), "rt": sb(512, F32), "yl": sb(512, F32), "yi": sb(512, F32),
 }
 for _i in range(8):
     SCRATCH["ps%d" % _i] = ("psum", [128, 512], F32)
@@ -158,66 +159,54 @@ def rank_program(g, core, T, topo):
     ps = [T["ps%d" % i] for i in range(8)]
 
     dma("s", T.lbuf[:], T.lett[:], [], ["lbuf"])
+    dma("a", T.tbuf[:], T.tid[:], [], ["tbuf"])
     dma("a", T.kx[:, 0:6, :], T.kid[0::2, :], [], ["kx0"])
     dma("s", T.kx[:, 6:12, :], T.kid[1::2, :], [], ["kx1"])
-    dma("a", T.tbuf[:], T.tid[:], [], ["tbuf"])
+    dma("s", T.tin[me], T.tid[2 * me:2 * me + 2, :], [], ["tin%d" % me])
     dma("s", T.lin[me], T.lett[2 * me:2 * me + 2, :], [], ["lin%d" % me])
-    dma("a", T.tin[me], T.tid[2 * me:2 * me + 2, :], [], ["tin%d" % me])
 
     def iota(key, out, pattern, base, mult):
         comp("g", [], [key], lambda: g.iota(out, pattern, base, mult, allow_small_or_imprecise_dtypes=True))
 
     comp("g", [], ["pi"], lambda: g.iota(T.pi[:], [[1, 1]], 0, 1))
-    iota("imk", T.imk[:], [[1, 128]], 0, -1)
-    iota("frk", T.frk[:], [[0, 4], [64, 2], [1, 16]], 0, -1)
-    iota("ix", T.ix[:], [[1, 143]], 0, 0)
+    iota("imk", T.imk[:], [[1, 143]], 0, -1)
     iota("e8i", T.e8i[0:8, :], [[1, 8], [0, 16]], 0, -1)
 
-    send("l", "sl", lambda q: T.lbuf[q], T.lin[me], ["lbuf"])
+    V([], ["tz0"], lambda: v.memset(T.tw[:, 0:1024], 0.0))
+    act(["tz0"], ["tz1"], T.tw[:, 1024:1536], T.tw[:, 0:512])
+    V(["imk"], ["ih"], lambda: v.tensor_scalar(T.ih[:], T.imk[:, 0:128], 0.0, None, A.is_equal))
+    V(["pi"], ["pci"], lambda: v.tensor_scalar(T.pci[:], T.pi[:], 15, None, A.bitwise_and))
+    V(["pi"], ["f1"], lambda: v.tensor_scalar(T.f1[:], T.pi[:], 15.0, 15.0, A.mult, A.add))
+    V(["pci"], ["pcf"], lambda: v.tensor_copy(T.pcf[:], T.pci[:]))
+
     send("t", "st", lambda q: T.tbuf[q], T.tin[me], ["tbuf"])
+    send("l", "sl", lambda q: T.lbuf[q], T.lin[me], ["lbuf"])
     for q in others:
         arrive("rl%d" % q, got(q), ["lin%d" % q])
         arrive("rt%d" % q, got(q), ["tin%d" % q])
-    iota("f8i", T.f8i[0:8, :], [[1, 143]], -15, -16)
-    iota("own16", T.own16[:], [[M, 4], [0, 4]], 0, 0)
+    iota("frk", T.frk[:], [[0, 4], [64, 2], [1, 16]], 0, -1)
     comp("g", [], ["expi"], lambda: g.iota(T.expi[:], [[1, 16]], 0, 0))
+    iota("kk", T.kk[:], [[1, 3]], 2, 0)
 
-    comp("a", ["imk"], ["tz0"], lambda: g.scalar.activation(T.tw[:, 0:128], T.imk[:], F.Copy, scale=0.0))
-    tz = ["tz0"]
-    for a, b in ((128, 256), (256, 512), (512, 1024), (1024, 2048), (2048, 3072)):
-        act(list(tz), ["tz%d" % a], T.tw[:, a:b], T.tw[:, 0:b - a])
-        tz.append("tz%d" % a)
+    def cast(q, la, hf):
+        o = T.kh[:, 3 * hf:3 * hf + 3, 64 * la:64 * la + 64]
+        i = T.kx[:, 6 * la + 3 * hf:6 * la + 3 * hf + 3, :]
+        if q == "v":
+            V(["kx%d" % la], ["kh%d%d" % (la, hf)], lambda: v.tensor_copy(o, i))
+        else:
+            act(["kx%d" % la], ["kh%d%d" % (la, hf)], o, i)
 
-    V(["pi"], ["pci"], lambda: v.tensor_scalar(T.pci[:], T.pi[:], 15, None, A.bitwise_and))
-    V(["pi"], ["pgi"], lambda: v.tensor_scalar(T.pgi[:], T.pi[:], 112, None, A.bitwise_and))
-    V(["pi"], ["poi"], lambda: v.tensor_scalar(T.poi[:], T.pi[:], 12, None, A.bitwise_and))
-    V(["pci"], ["pcf"], lambda: v.tensor_copy(T.pcf[:], T.pci[:]))
-    V(["pgi"], ["k16"], lambda: v.tensor_scalar(T.k16[:], T.pgi[:], 15.0, None, A.add))
-    V(["poi"], ["own1"], lambda: v.tensor_scalar(T.own1[:], T.poi[:], 192.0, None, A.mult))
-    V(["imk"], ["ih"], lambda: v.tensor_scalar(T.ih[:], T.imk[:], 0.0, None, A.is_equal))
-    V(["pcf"], ["npc"], lambda: v.tensor_scalar(T.npc[:], T.pcf[:], -1.0, None, A.mult))
-    V(["pcf"], ["wab"], lambda: v.tensor_scalar(T.wab[:], T.pcf[:], 2.0, None, A.is_lt))
-    V(["pcf"], ["wf"], lambda: v.tensor_scalar(T.wf[:], T.pcf[:], 2.0, K17, A.is_equal, A.mult))
-    V(["imk"], ["ib"], lambda: v.tensor_scalar(T.ib[:], T.imk[:], 0.0, None, A.is_equal))
-    V(["imk"], ["shb"], lambda: v.tensor_scalar(T.shb[:], T.imk[:], 3.0, None, A.is_equal))
-    for n in range(4):
-        V(["frk"], ["r%d" % n], lambda: v.tensor_scalar(T["r%d" % n][:], T.frk[:], float(-16 * n), None, A.is_equal))
-    for nm in ("t1b", "t1h"):
-        V(["ix", "k16"], [nm], lambda: v.tensor_scalar(T[nm][:], T.ix[:], T.k16[:], None, A.is_equal))
-    V(["e8i"], ["e8"], lambda: v.tensor_scalar(T.e8[0:8, :], T.e8i[0:8, :], 0.0, None, A.is_equal))
-
+    for q, la, hf in (("v", 0, 0), ("a", 0, 1), ("v", 1, 0), ("a", 1, 1)):
+        cast(q, la, hf)
     for hf in range(2):
-        for la in range(2):
-            V(["kx%d" % la], ["kh%d%d" % (la, hf)],
-              lambda: v.tensor_copy(T.kh[:, 3 * hf:3 * hf + 3, 64 * la:64 * la + 64],
-                                    T.kx[:, 6 * la + 3 * hf:6 * la + 3 * hf + 3, :]))
-    for b in range(6):
-        comp("t", ["kh0%d" % (b // 3), "kh1%d" % (b // 3), "ih"], ["ps%d" % (b // 2)],
-             lambda: pe.matmul(ps[b // 2][:, 128 * (b % 2):128 * (b % 2) + 128], T.kh[:, b, :], T.ih[:], True, True))
-    for b in range(6):
-        V(["ps%d" % (b // 2)], ["ks%d" % b],
-          lambda: v.tensor_copy(T.ks[:, b::6], ps[b // 2][:, 128 * (b % 2):128 * (b % 2) + 128]))
-    ksk = ["ks%d" % b for b in range(6)]
+        for x in range(2):
+            comp("t", ["kh0%d" % hf, "kh1%d" % hf, "ih"], ["ps%d" % x],
+                 [lambda b=b: pe.matmul(ps[x][:, b:384:6], T.kh[:, b, :], T.ih[:, 64 * x:64 * x + 64], True, True)
+                  for b in range(3 * hf, 3 * hf + 3)])
+    code = float(M * me) - OFF
+    V(["ps0"], ["ks0"], lambda: v.tensor_scalar(T.ks[:, 0:384], ps[0][:, 0:384], code, None, A.add))
+    comp("a", ["ps1"], ["ks1"], lambda: g.scalar.activation(T.ks[:, 384:768], ps[1][:, 0:384], F.Copy, bias=code))
+    ksk = ["ks0", "ks1"]
     eng = topo.engines(core, cores[near[0]])
     ways = ([(near[0], eng[:len(eng) // 2]), (near[1], eng[len(eng) // 2:])], [(near[2], eng)])
     deps("g", ksk, [])
@@ -229,58 +218,64 @@ def rank_program(g, core, T, topo):
     for q in others:
         arrive("rk%d" % q, len(eng) if q == near[2] else len(eng) // 2, ["kin%d" % q])
 
+    iota("tz2", T.tw[:, 1536:3072], [[0, 1536]], 0, 0)
+    tz = ["tz0", "tz1", "tz2"]
+    iota("one", T.one[:], [[0, 128]], 1, 0)
+    comp("g", ["one"], ["ib"], lambda: g.affine_select(T.ib[:], T.one[:], [[1, 128]], A.is_equal, 0.0, 0, -1))
+    comp("g", ["one"], ["shb"], lambda: g.affine_select(T.shb[:], T.one[:], [[1, 128]], A.is_equal, 0.0, -3, -1))
+
     lins = ["lin%d" % q for q in range(4)]
     tins = ["tin%d" % q for q in range(4)]
-    dma("s", T.lu[0:8, 0:1024], T.lin[:], lins, ["lua"])
-    dma("s", T.lu[0:6, 1024:1040], T.lin[1:4, 0::64, :], lins, ["lub"])
-    dma("s", T.lu[6:8, 1024:1040], T.lin[0, 0::64, :], lins, ["luc"])
     for la in range(2):
         dma("s", T.ht[32 * la:32 * la + 32, :], T.tin[:, 64 * la:64 * la + 64, :], tins, ["ht%d" % la])
+    dma("s", T.li[0:8, 0:1024], T.lin[:], lins, ["lia"])
+    dma("s", T.li[0:6, 1024:1040], T.lin[1:4, 0::64, :], lins, ["lib"])
+    dma("s", T.li[6:8, 1024:1040], T.lin[0, 0::64, :], lins, ["lic"])
 
-    V(["f8i"], ["f8"], lambda: v.tensor_scalar(T.f8[0:8, :], T.f8i[0:8, :], 0.0, None, A.is_equal))
-    V(["f8i"], ["f8s"], lambda: v.tensor_scalar(T.f8s[0:8, :], T.f8i[0:8, :], 0.0, 16.0, A.is_equal, A.mult))
-
-    def spread(q, bank):
+    def spread(q, ka, kb, va):
         src, keys = (T.ks, ksk) if q == me else (T.kin, ["kin%d" % q])
-        for half in range(2):
-            k = bank + half
-            for j in range(2):
-                comp("t", keys + ["r%d" % (2 * half + j)], ["ps%d" % k],
-                     lambda: pe.matmul(ps[k][:, 192 * j:192 * j + 192], T["r%d" % (2 * half + j)][:],
-                                       src[:, 192 * q:192 * q + 192], True, True))
-            for j in range(2):
-                n = 2 * half + j
-                o = T.win[:, M * q + n:M * q + M:4]
-                i = ps[k][:, 192 * j:192 * j + 192]
-                if half == 0:
-                    V(["ps%d" % k], ["w%d%d" % (q, n)], lambda: v.tensor_copy(o, i))
-                else:
-                    act(["ps%d" % k], ["w%d%d" % (q, n)], o, i)
+        c = 192 * q
+        for k, a, b in ((ka, 0, va // 4), (kb, va // 4, 192)):
+            comp("t", keys + ["r%d" % n for n in range(4)], ["ps%d" % k],
+                 [lambda n=n: pe.matmul(ps[k][:, n:4 * (b - a):4], T["r%d" % n][:], src[:, c + a:c + b], True, True)
+                  for n in range(4)])
+        V(["ps%d" % ka], ["wa%d" % q], lambda: v.tensor_copy(T.win[:, M * q:M * q + va], ps[ka][:, 0:va]))
+        act(["ps%d" % kb], ["wb%d" % q], T.win[:, M * q + va:M * q + M], ps[kb][:, 0:M - va])
 
-    spread(me, 4)
+    for n in range(4):
+        V(["frk"], ["r%d" % n], lambda: v.tensor_scalar(T["r%d" % n][:], T.frk[:], float(-16 * n), None, A.is_equal))
+    spread(me, 4, 5, SA)
 
-    for k in (2, 3, 4):
-        V(["wf", "wab"], ["w%d" % k],
-          lambda: v.tensor_scalar(T["w%d" % k][:], T.wf[:], float(k), T.wab[:], A.mult, A.add))
+    V(["e8i"], ["e8"], lambda: v.tensor_scalar(T.e8[0:8, :], T.e8i[0:8, :], 0.0, None, A.is_equal))
+    V(["imk", "f1"], ["f8"], lambda: v.tensor_scalar(T.f8[0:8, :], T.imk[0:8, :], T.f1[0:8, :], None, A.is_equal))
+    V(["imk", "f1"], ["f8s"],
+      lambda: v.tensor_scalar(T.f8s[0:8, :], T.imk[0:8, :], T.f1[0:8, :], 16.0, A.is_equal, A.mult))
+    V(["pcf"], ["k16"], lambda: v.tensor_scalar(T.k16[:], T.pcf[:], -1.0, 15.0, A.mult, A.add))
+    V(["pi"], ["poi"], lambda: v.tensor_scalar(T.poi[:], T.pi[:], 12, None, A.bitwise_and))
+    V(["pcf"], ["wab"], lambda: v.tensor_scalar(T.wab[:], T.pcf[:], 2.0, None, A.is_lt))
+    V(["pcf"], ["wf"], lambda: v.tensor_scalar(T.wf[:], T.pcf[:], 2.0, K17, A.is_equal, A.mult))
     V(["pcf"], ["wg"], lambda: v.tensor_scalar(T.wg[:], T.pcf[:], 3.0, None, A.is_ge))
     V(["pcf"], ["wh"], lambda: v.tensor_scalar(T.wh[:], T.pcf[:], 5.0, K17 - 1.0, A.is_ge, A.mult))
+    V(["poi"], ["own1"], lambda: v.tensor_scalar(T.own1[:], T.poi[:], 192.0, OFF, A.mult, A.add))
+    V(["imk", "k16"], ["t1h"], lambda: v.tensor_scalar(T.t1h[:], T.imk[:], T.k16[:], None, A.is_equal))
+    V(["kk", "wf", "wab"], ["wk"],
+      lambda: v.tensor_scalar(T.wk[:], T.kk[:], T.wf[:], T.wab[:], A.mult, A.add))
     V(["wg", "wh"], ["w1"], lambda: v.tensor_tensor(T.w1[:], T.wg[:], T.wh[:], A.add))
-    for k in (2, 3, 4, 1):
-        comp("a", ["t1b", "w%d" % k], ["tw_%d" % k],
-             lambda: g.scalar.activation(T["tw%d" % k][:], T.t1b[:], F.Identity, scale=T["w%d" % k][:]))
+    V(["imk"], ["id"], lambda: v.tensor_scalar(T["id"][:], T.imk[:, 0:128], 0.0, None, A.is_equal))
     V(["expi"], ["expu"], lambda: v.tensor_copy(T.expu[:], T.expi[:]))
+    for j, w in enumerate((T.wk[:, 0:1], T.w1[:], T.wk[:, 1:2], T.wk[:, 2:3])):
+        V(["imk", "k16", "w1", "wk"], ["vt%d" % j],
+          lambda: v.tensor_scalar(T.vt[:, 8 * j:8 * j + 8], T.imk[:, 15:143:16], T.k16[:], w, A.is_equal, A.mult))
 
-    V(["lua"], ["uha"], lambda: v.tensor_copy(T.uh[0:8, 0:512], T.lu[0:8, 0:512]))
-    V(["lua", "lub", "luc"], ["uhb"], lambda: v.tensor_copy(T.uh[0:8, 512:1040], T.lu[0:8, 512:1040]))
-    for k, a, b, uk in ((1, 0, 512, "uha"), (0, 512, 1024, "uhb"), (2, 1024, 1040, "uhb")):
-        comp("t", [uk, "e8"], ["ps%d" % k],
-             lambda: pe.matmul(ps[k][:, 0:b - a], T.e8[0:8, :], T.uh[0:8, a:b], True, True))
-    comp("a", ["ps1", "npc"], ["ea"], lambda: g.scalar.activation(T.ea[:], ps[1][:, 0:512], F.Abs, bias=T.npc[:]))
-    comp("a", ["ea"], ["em1"], lambda: g.scalar.activation(T.em[:, 0:512], T.ea[:], F.Relu, bias=1.0, scale=-1.0))
+    for q, (ka, kb) in zip(near[:2], ((6, 7), (4, 5))):
+        spread(q, ka, kb, SB)
+
+    V(["lia"], ["lua"], lambda: v.tensor_copy(T.lu[0:8, 0:512], T.li[0:8, 0:512]))
+    act(["lia", "lib", "lic"], ["lub"], T.lu[0:8, 512:1040], T.li[0:8, 512:1040])
 
     hts = ["ht0", "ht1"]
     V(hts, ["hb0"], lambda: v.tensor_copy(T.hb[0:64, 0:96], T.ht[0:64, :]))
-    V(hts, ["hb2"], lambda: v.tensor_scalar(T.hb[0:64, 192:288], T.ht[0:64, :], 1.0, None, A.min))
+    comp("a", hts, ["hb2"], lambda: g.scalar.activation(T.hb[0:64, 192:288], T.ht[0:64, :], F.Sign))
     V(hts + ["hb0"], ["hb1"], lambda: v.tensor_tensor(T.hb[0:64, 96:192], T.ht[0:64, :], T.hb[0:64, 0:96], A.subtract))
     tws = []
     for x in (0, 2, 1):
@@ -288,102 +283,124 @@ def rank_program(g, core, T, topo):
             deps("s", tz, [])
             dma("s", T.tw[32 * s + x:32 * s + 32:16, :], T.hb[0:64, 96 * x:96 * x + 96], ["hb%d" % x], ["tw%d%d" % (x, s)])
             tws.append("tw%d%d" % (x, s))
-    for k, a, b in ((0, 512, 1024), (2, 1024, 1040)):
+
+    def mask(k, a, b):
         V(["ps%d" % k, "pcf"], ["em%d" % k],
           lambda: v.tensor_scalar(T.em[:, a:b], ps[k][:, 0:b - a], T.pcf[:], None, A.is_equal))
-    ems = ["em0", "em1", "em2"]
 
-    for q, bank in zip(near, (6, 4, 1)):
-        spread(q, bank)
+    for k, a, b, uk in ((2, 0, 512, "lua"), (3, 512, 1024, "lub"), (0, 1024, 1040, "lub")):
+        comp("t", [uk, "e8"], ["ps%d" % k],
+             lambda: pe.matmul(ps[k][:, 0:b - a], T.e8[0:8, :], T.lu[0:8, a:b], True, True))
+    mask(2, 0, 512)
+    mask(0, 1024, 1040)
+
+    spread(near[2], 6, 7, SB)
     calls = []
     for i in range(16):
-        calls.append(lambda i=i: pe.matmul(ps[3][:, 0:64], T.f8s[0:8, 15 - i:143 - i], T.uh[0:8, i:1024:16], i == 0, False))
-        calls.append(lambda i=i: pe.matmul(ps[3][:, 0:64], T.f8[0:8, 15 - i:143 - i], T.uh[0:8, i + 1:i + 1010:16], False,
+        calls.append(lambda i=i: pe.matmul(ps[1][:, 0:64], T.f8s[0:8, 15 - i:143 - i], T.lu[0:8, i:1024:16], i == 0, False))
+        calls.append(lambda i=i: pe.matmul(ps[1][:, 0:64], T.f8[0:8, 15 - i:143 - i], T.lu[0:8, i + 1:i + 1010:16], False,
                                            i == 15))
-    comp("t", ["uha", "uhb", "f8", "f8s"], ["ps3"], calls)
+    comp("t", ["lua", "lub", "f8", "f8s"], ["ps1"], calls)
+    act(["ps1"], ["cu"], T.cu[:], ps[1][:, 0:64])
 
-    wk = ["w%d%d" % (q, n) for q in range(4) for n in range(4)]
-    V(wk, ["n1s"], lambda: v.tensor_reduce(T.n1s[:], T.win[:, 1::M], AxisListType.X, A.add))
+    wk = ["w%s%d" % (x, q) for q in range(4) for x in "ab"]
+    win = T.win[:, 0:3072]
+    twin = T.tw[:, 0:3072]
+    V(["wa%d" % q for q in range(4)], ["n1s"], lambda: v.tensor_reduce(T.n1s[:], T.win[:, 1::M], AxisListType.X, A.add))
     V(["n1s", "own1"], ["n1u"], lambda: v.tensor_scalar(T.n1u[:, 0:1], T.n1s[:], T.own1[:], None, A.add))
-    V(wk + ["n1u", "own16"], ["n2f"],
-      lambda: v.tensor_tensor(T.n2f[:], T.win[:, 0:3072].indirect(T.n1u[:, 0:1]), T.own16[:], A.add))
-    V(["n2f"], ["n2u"], lambda: v.tensor_copy(T.n2u[:], T.n2f[:]))
-    V(wk + ["n2u"], ["nw"], lambda: v.tensor_copy(T.nw[:], T.win[:, 0:3072].indirect(T.n2u[:, 0:16])))
-    V(["ps3"], ["cu"], lambda: v.tensor_copy(T.cu[:], ps[3][:, 0:64]))
+    V(wk + ["n1u"], ["n2u"], lambda: v.tensor_scalar(T.n2u[:], win.indirect(T.n1u[:, 0:1]), OFF, None, A.add))
+    V(wk + ["n2u"], ["nw"], lambda: v.tensor_copy(T.nw[:], win.indirect(T.n2u[:, 0:16])))
 
-    act(tws + ["n1u"], ["g1"], T.g1[:], T.tw[:, 0:3072].indirect(T.n1u[:, 0:1]))
+    act(tws + ["n1u"], ["g1"], T.g1[:], twin.indirect(T.n1u[:, 0:1]))
     act(["g1", "expu"], ["g1e"], T.g1e[:], T.g1[:, 0:16].indirect(T.expu[:, 0:16]))
-    act(tws + ["n2u"], ["g2"], T.g2[:], T.tw[:, 0:3072].indirect(T.n2u[:, 0:16]))
+    act(tws + ["n2u"], ["g2"], T.g2[:], twin.indirect(T.n2u[:, 0:16]))
+
+    portions = ((0, CUT), (CUT, 1024))
+
+    def walk(p, h, w, lst, e, R):
+        a, b = portions[h]
+        V(R + ["em2", "em0"] + (["em3"] if h else []), ["%s%d" % (p, h)],
+          lambda: v.tensor_tensor(T[p][:, a:b], w.indirect(lst[:, a // 16:b // 16]), T.em[:, a + e:b + e], A.mult))
+
+    def nodes(bank, p, h):
+        a, b = portions[h]
+        comp("t", ["%s%d" % (p, h), "t1h"], ["ps%d" % bank],
+             [lambda i=i: pe.matmul(ps[bank][:, 0:(b - a) // 16], T.t1h[:, 15 - i:143 - i], T[p][:, a + i:b:16], i == 0,
+                                    i == 15) for i in range(16)])
+
+    def lists(bank, nm, h):
+        a, b = portions[h]
+        V(["ps%d" % bank], ["%s%d" % (nm, h)],
+          lambda: v.tensor_scalar(T[nm][:, a // 16:b // 16], ps[bank][:, 0:(b - a) // 16], OFF, None, A.add))
+
+    pieces = {"i12": [], "i3": [], "i4": []}
+
+    def ids(q, rep, w, lst, a, b, R):
+        key = "%s_%d" % (rep, a)
+        pieces[rep].append((key, a, b))
+        i = w.indirect(lst[:, a // 16:b // 16])
+        if q == "v":
+            V(R, [key], lambda: v.tensor_copy(T[rep][:, a:b], i))
+        else:
+            act(R, [key], T[rep][:, a:b], i)
+
+    def value(rep, bank, n, j, lo, hi):
+        for c in range(lo, hi):
+            keys = [k for k, a, b in pieces[rep] if a < 128 * c + 128 and 128 * c < b]
+            comp("t", keys + ["vt%d" % (j + x) for x in range(n)], ["ps%d" % bank],
+                 lambda: pe.matmul(ps[bank][:, c:64 * n:8], T[rep][:, 128 * c:128 * c + 128], T.vt[:, 8 * j:8 * j + 8 * n],
+                                   True, True))
+
+    walk("p3", 0, T.nw[:, 0:256], T.cu, 2, ["nw", "cu"])
+    nodes(4, "p3", 0)
     comp("t", ["g1e", "g2", "shb", "ib"], ["ps0"],
          [lambda: pe.matmul(ps[0][:, 0:256], T.shb[:], T.g1e[:], True, False),
           lambda: pe.matmul(ps[0][:, 0:256], T.ib[:], T.g2[:], False, True)])
     act(["ps0"], ["g12"], T.g12[:], ps[0][:, 0:256])
-
-    def nodes(bank, p):
-        calls = []
-        for i in range(16):
-            calls.append(lambda i=i: pe.matmul(ps[bank][:, 0:64], T.t1h[:, 15 - i:143 - i], T[p][:, i::16], i == 0, False))
-        comp("t", [p, "t1h"], ["ps%d" % bank], calls)
-        comp("t", ["ownl", "ih"], ["ps%d" % bank], lambda: pe.matmul(ps[bank][:, 0:64], T.ih[:], T.ownl[:], False, True))
-
-    def value(k, bank, rep, keys, lo, hi, first, last):
-        calls = []
-        for i in range(lo, hi):
-            calls.append(lambda i=i: pe.matmul(ps[bank][:, 0:64], T["tw%d" % k][:, 15 - i:143 - i],
-                                               T[rep][:, 64 * i:64 * i + 64], first and i == lo, last and i == hi - 1))
-        comp("t", keys + ["tw_%d" % k], ["ps%d" % bank], calls)
-
-    V(["nw", "cu"] + ems, ["p3"],
-      lambda: v.tensor_tensor(T.p3[:], T.nw[:, 0:256].indirect(T.cu[:, 0:64]), T.em[:, 2:1026], A.mult))
-    V(["ps3"], ["ci"], lambda: v.tensor_copy(T.ci[:], ps[3][:, 0:64]))
-    V(["ci"], ["oi"], lambda: v.tensor_scalar(T.oi[:], T.ci[:], 6, None, A.arith_shift_right))
-    V(["oi"], ["ownl"], lambda: v.tensor_scalar(T.ownl[:], T.oi[:], float(M), None, A.mult))
-    nodes(7, "p3")
-    V(["ps7"], ["n3u"], lambda: v.tensor_copy(T.n3u[:], ps[7][:, 0:64]))
-    act(["g12", "cu"], ["i12a"], T.i12[:, 0:512], T.g12[:, 0:256].indirect(T.cu[:, 0:32]))
-    act(["g12", "cu"], ["i12b"], T.i12[:, 512:1024], T.g12[:, 0:256].indirect(T.cu[:, 32:64]))
-    V(wk + ["n3u"] + ems, ["p4"],
-      lambda: v.tensor_tensor(T.p4[:], T.win[:, 0:3072].indirect(T.n3u[:, 0:64]), T.em[:, 3:1027], A.mult))
-    act(tws + ["n3u"], ["i3"], T.i3[:], T.tw[:, 0:3072].indirect(T.n3u[:, 0:64]))
-    for hf in range(2):
-        for k, bank in ((2, 1), (1, 4)):
-            value(k, bank, "i12", ["i12%s" % "ab"[hf]], 8 * hf, 8 * hf + 8, hf == 0, hf == 1)
-    V(["ps4"], ["b1"], lambda: v.tensor_copy(T.b1[:], ps[4][:, 0:64]))
+    mask(3, 512, 1024)
+    walk("p3", 1, T.nw[:, 0:256], T.cu, 2, ["nw", "cu"])
+    nodes(5, "p3", 1)
+    for a in (0, 512):
+        ids("a", "i12", T.g12[:, 0:256], T.cu, a, a + 512, ["g12", "cu"])
+    for h in range(2):
+        lists(4 + h, "n3u", h)
+        walk("p4", h, win, T.n3u, 3, wk + ["n3u%d" % h])
+        nodes(6 + h, "p4", h)
+        ids("a", "i3", twin, T.n3u, portions[h][0], portions[h][1], tws + ["n3u%d" % h])
+    value("i12", 1, 2, 0, 0, 8)
+    value("i3", 3, 1, 2, 0, 8)
+    lists(6, "n4u", 0)
+    ids("v", "i4", twin, T.n4u, 0, CUT, tws + ["n4u0"])
+    lists(7, "n4u", 1)
+    V(["ps1"], ["b1"], lambda: v.tensor_copy(T.b1[:], ps[1][:, 64:128]))
+    ids("v", "i4", twin, T.n4u, CUT, 768, tws + ["n4u1"])
+    ids("a", "i4", twin, T.n4u, 768, 1024, tws + ["n4u1"])
     V(["ps1", "b1"], ["b2"], lambda: v.tensor_tensor(T.b2[:], ps[1][:, 0:64], T.b1[:], A.max))
-    nodes(2, "p4")
-    V(["ps2"], ["n4u"], lambda: v.tensor_copy(T.n4u[:], ps[2][:, 0:64]))
-    for x in range(2):
-        for y in range(2):
-            q = 2 * y + x
-            o = T.i4[:, 256 * q:256 * q + 256]
-            i = T.tw[:, 0:3072].indirect(T.n4u[:, 16 * q:16 * q + 16])
-            if y == 0:
-                V(tws + ["n4u"], ["i4%d" % q], lambda: v.tensor_copy(o, i))
-            else:
-                act(tws + ["n4u"], ["i4%d" % q], o, i)
-    value(3, 5, "i3", ["i3"], 0, 16, True, True)
-    for n, q in enumerate((0, 2, 1, 3)):
-        value(4, 6, "i4", ["i4%d" % q], 4 * q, 4 * q + 4, n == 0, n == 3)
-    V(["ps5", "b2"], ["b3"], lambda: v.tensor_tensor(T.b3[:], ps[5][:, 0:64], T.b2[:], A.max))
-    mc = slice(64 * me, 64 * me + 64)
-    V(["ps6", "b3"], ["res%d" % me], lambda: v.tensor_tensor(T.res[:, mc], ps[6][:, 0:64], T.b3[:], A.max))
+    value("i4", 0, 1, 3, 0, 8)
+    V(["ps3", "b2"], ["b3"], lambda: v.tensor_tensor(T.b3[:], ps[3][:, 0:64], T.b2[:], A.max))
+    V(["ps0", "b3"], ["res"], lambda: v.tensor_tensor(T.res[:], ps[0][:, 0:64], T.b3[:], A.max))
 
-    deps("g", ["res%d" % me], [])
-    g.remote_dma_fused([RemoteDMATransfer(dst_ids=[dst(cores[q]) for q in others], dma_engine_mask=bits(eng),
-                                          remote_sem=T.sem["rr%d" % me], srcs=[T.res[:, mc]],
-                                          dsts=[T.res[:, mc] for q in others])], local_sem=T.sem.sr)
-    total["sr"] = len(eng)
+    deps("g", ["res"], [])
+    total["sr"] = 0
+    for way in ways:
+        g.remote_dma_fused([RemoteDMATransfer(dst_ids=[dst(cores[q])], dma_engine_mask=bits(e), remote_sem=T.sem["rr%d" % me],
+                                              src=T.res[:, 16 * q:16 * q + 16], dst=T.rcv[:, 16 * me:16 * me + 16])
+                            for q, e in way], local_sem=T.sem.sr)
+        total["sr"] += len(eng)
     for q in others:
-        arrive("rr%d" % q, len(topo.engines(cores[q], core)), ["res%d" % q])
-    pr = slice(32 * me, 32 * me + 32)
-    for q in [me] + near:
-        c = slice(64 * q, 64 * q + 64)
-        V(["res%d" % q], ["rt%d" % q], lambda: v.tensor_scalar(T.rt[pr, c], T.res[pr, c], RND, RND, A.add, A.subtract))
-        V(["res%d" % q, "rt%d" % q], ["yi%d" % q],
-          lambda: v.tensor_tensor(T.yi[pr, c], T.res[pr, c], T.rt[pr, c], A.subtract))
-        comp("a", ["rt%d" % q], ["yl%d" % q], lambda: g.scalar.activation(T.yl[pr, c], T.rt[pr, c], F.Copy, scale=1.0 / K17))
-        dma("s", T.yid[2 * q:2 * q + 2, :], T.yi[pr, c], ["yi%d" % q], ["oi%d" % q])
-        dma("a", T.ylen[2 * q:2 * q + 2, :], T.yl[pr, c], ["yl%d" % q], ["ol%d" % q])
+        arrive("rr%d" % q, len(eng) if q == near[2] else len(eng) // 2, ["rcv%d" % q])
+    for q, bank in zip([me] + near, (4, 5, 6, 7)):
+        i, key = (T.res, "res") if q == me else (T.rcv, "rcv%d" % q)
+        c = slice(128 * q, 128 * q + 128)
+        p = ps[bank][0:16, 0:128]
+        comp("t", [key, "id"], ["ps%d" % bank], lambda: pe.transpose(p, i[:, 16 * q:16 * q + 16], T["id"][:]))
+        V(["ps%d" % bank], ["rt%d" % q], lambda: v.tensor_scalar(T.rt[0:16, c], p, RND, RND, A.add, A.subtract))
+        V(["ps%d" % bank, "rt%d" % q], ["yi%d" % q],
+          lambda: v.tensor_tensor(T.yi[0:16, c], p, T.rt[0:16, c], A.subtract))
+        comp("a", ["rt%d" % q], ["yl%d" % q],
+             lambda: g.scalar.activation(T.yl[0:16, c], T.rt[0:16, c], F.Copy, scale=1.0 / K17))
+        dma("s", T.yid[2 * q:2 * q + 2, :], T.yi[0:16, c], ["yi%d" % q], ["oi%d" % q])
+        dma("a", T.ylen[2 * q:2 * q + 2, :], T.yl[0:16, c], ["yl%d" % q], ["ol%d" % q])
 
     for s in total:
         if seen.get(s, 0) < total[s]:

@@ -1,12 +1,13 @@
 import numpy as np
 from concourse.bass import DstId, RemoteDMATransfer
-from concourse.mybir import AluOpType as A, AxisListType, ActivationFunctionType as F
+from concourse.mybir import AluOpType as A, ActivationFunctionType as F
 
 NR = 4
 M = 768
 OFF = 1536.0
-SA, SB = 448, 384
+SA, SF, SN, SM = 320, 256, 256, 352
 CUT = 480
+IV = 832
 K17 = 131072.0
 RND = 12582912.0 * K17
 HF = "float16"
@@ -21,32 +22,31 @@ def sb(cols, dtype):
 
 
 SCRATCH = {
-    "lbuf": ("dram", [4, 128, 16], I32), "lin": ("dram", [4, 128, 16], I32),
+    "lbuf": ("dram", [4, 128, 16], HF), "lin": ("dram", [4, 128, 16], HF),
     "tbuf": ("dram", [4, 128, 12], I32), "tin": ("dram", [4, 128, 12], I32),
-    "kx": sb([12, 64], I32), "kh": sb([6, 128], HF), "ks": sb(768, HF), "kin": sb(768, HF),
+    "lx": sb(64, I32), "lf": sb(64, HF), "kx": sb([12, 64], I32), "kh": sb([6, 128], HF),
+    "ks": sb(768, HF), "kin": sb(768, HF),
     "win": sb(3072, F32), "tw": sb(3072, BF), "nw": sb(256, F32),
-    "ht": sb(96, I32), "hb": sb(288, BF),
-    "li": sb(1040, I32), "lu": sb(1040, BF), "em": sb(1040, BF),
-    "pi": sb(1, I32), "pci": sb(1, I32), "poi": sb(1, I32),
-    "pcf": sb(1, F32), "k16": sb(1, F32), "own1": sb(1, F32), "f1": sb(1, F32),
-    "imk": sb(143, BF), "frk": sb(128, BF), "e8i": sb(128, BF), "one": sb(128, BF), "kk": sb(3, F32),
+    "ht": sb(192, I32), "hb": sb(576, BF),
+    "lu": sb(1040, HF), "ll": sb(136, HF), "em": sb(1072, BF),
+    "pi": sb(1, I32), "pci": sb(1, I32),
+    "pcf": sb(1, F32), "k16": sb(1, F32), "zz": sb(1, F32), "sa": sb(1, F32), "sk": sb(1, F32),
+    "imk": sb(143, BF), "frk": sb(128, BF), "e8i": sb(128, BF), "pdi": sb(128, BF), "one": sb(128, BF),
     "expi": sb(16, I32), "expu": sb(16, U16),
-    "e8": sb(128, BF), "f8": sb(143, BF), "f8s": sb(143, BF),
+    "e8": sb(128, HF), "ih": sb(128, HF), "i16": sb(128, HF), "sh1": sb(128, HF),
     "r0": sb(128, HF), "r1": sb(128, HF), "r2": sb(128, HF), "r3": sb(128, HF),
-    "ih": sb(128, HF), "id": sb(128, F32), "ib": sb(128, BF), "shb": sb(128, BF), "t1h": sb(143, HF),
-    "wab": sb(1, F32), "wf": sb(1, F32), "wg": sb(1, F32), "wh": sb(1, F32), "w1": sb(1, F32), "wk": sb(3, F32),
-    "vt": sb(32, BF),
-    "cu": sb(64, U16), "n1s": sb(1, F32), "n1u": sb(2, U16), "n2u": sb(16, U16), "n3u": sb(64, U16), "n4u": sb(64, U16),
+    "id": sb(128, F32), "ib": sb(128, BF), "shb": sb(128, BF), "t1h": sb(143, HF), "vt": sb(32, BF),
+    "cu": sb(64, U16), "n1u": sb(8, U16), "n2u": sb(64, U16), "n3u": sb(64, U16), "n4u": sb(64, U16),
     "p3": sb(1024, HF), "p4": sb(1024, HF),
-    "g1": sb(16, BF), "g1e": sb(256, BF), "g2": sb(256, BF), "g12": sb(256, BF),
+    "g1": sb(64, BF), "g1e": sb(256, BF), "g2": sb(256, BF), "g12": sb(256, BF),
     "i12": sb(1024, BF), "i3": sb(1024, BF), "i4": sb(1024, BF),
     "b1": sb(64, F32), "b2": sb(64, F32), "b3": sb(64, F32),
-    "res": sb(64, F32), "rcv": sb(64, F32), "rt": sb(512, F32), "yl": sb(512, F32), "yi": sb(512, F32),
+    "res": sb(64, F32), "rcv": sb(64, F32), "rt": sb(128, F32), "yl": sb(128, F32), "yi": sb(128, F32),
 }
 for _i in range(8):
     SCRATCH["ps%d" % _i] = ("psum", [128, 512], F32)
-SEMAPHORES = (["cv", "ca", "ct", "cg", "sl", "st", "sk0", "sk1", "sr"]
-              + ["r%s%d" % (x, i) for x in "ltkr" for i in range(NR)] + ["d%d" % i for i in range(48)])
+SEMAPHORES = (["cv", "ca", "ct", "cg", "sl", "st", "sr"]
+              + ["%s%d" % (x, i) for x in ("sk", "rl", "rt", "rk", "rr") for i in range(NR)] + ["d%d" % i for i in range(48)])
 
 
 def shares(topo, src, dsts):
@@ -73,9 +73,10 @@ def rank_program(g, core, T, topo):
         return
     cores = list(T.cores)
     others = [q for q in range(NR) if q != me]
-    near = [q for q in others if topo.mates(topo.chip(core), topo.chip(cores[q]))]
-    near += [q for q in others if topo.same_plane(topo.chip(core), topo.chip(cores[q]))]
-    near += [q for q in others if q not in near]
+    mate = [q for q in others if topo.mates(topo.chip(core), topo.chip(cores[q]))]
+    plane = [q for q in others if topo.same_plane(topo.chip(core), topo.chip(cores[q]))]
+    order = [q for q in others if q not in mate + plane] + plane + mate
+    f, n, m = order
     q_of = {"g": g, "v": g.vector, "a": g.scalar, "t": g.tensor, "s": g.sync}
     csem = {"g": "cg", "v": "cv", "a": "ca", "t": "ct"}
     total = {}
@@ -87,8 +88,8 @@ def rank_program(g, core, T, topo):
 
     def wait(q, evs):
         most = {}
-        for s, v in evs:
-            most[s] = max(v, most.get(s, 0))
+        for s, x in evs:
+            most[s] = max(x, most.get(s, 0))
         for s in most:
             if waited.get((q, s), 0) < most[s]:
                 q_of[q].wait_ge(T.sem[s], most[s])
@@ -133,8 +134,8 @@ def rank_program(g, core, T, topo):
         total[s] = 16
         note((s, 16), R, W)
 
-    def arrive(s, n, keys):
-        total[s] = total.get(s, 0) + n
+    def arrive(s, x, keys):
+        total[s] = total.get(s, 0) + x
         for k in keys:
             lastw[k] = [(s, total[s])]
 
@@ -144,12 +145,12 @@ def rank_program(g, core, T, topo):
 
     mine = shares(topo, core, [cores[q] for q in others])
 
-    def send(rsem, lsem, src_of, out, R):
+    def send(rsem, lsem, way, src_of, out, R):
         deps("g", R, [])
-        tr = [RemoteDMATransfer(dst_ids=[dst(cores[q])], dma_engine_mask=bits(mine[cores[q]]),
-                                remote_sem=T.sem["r%s%d" % (rsem, me)], src=src_of(q), dst=out) for q in others]
+        tr = [RemoteDMATransfer(dst_ids=[dst(cores[q])], dma_engine_mask=bits(e), remote_sem=T.sem["%s%d" % (rsem, me)],
+                                src=src_of(q), dst=out) for q, e in way]
         g.remote_dma_fused(tr, local_sem=T.sem[lsem])
-        total[lsem] = sum(len(mine[cores[q]]) for q in others)
+        total[lsem] = total.get(lsem, 0) + sum(len(e) for q, e in way)
 
     def got(q):
         return len(shares(topo, cores[q], [c for c in cores if c != cores[q]])[core])
@@ -158,169 +159,248 @@ def rank_program(g, core, T, topo):
     pe = g.tensor
     ps = [T["ps%d" % i] for i in range(8)]
 
-    dma("s", T.lbuf[:], T.lett[:], [], ["lbuf"])
-    dma("a", T.tbuf[:], T.tid[:], [], ["tbuf"])
-    dma("a", T.kx[:, 0:6, :], T.kid[0::2, :], [], ["kx0"])
-    dma("s", T.kx[:, 6:12, :], T.kid[1::2, :], [], ["kx1"])
+    def load(q):
+        p = slice(32 * q, 32 * q + 32)
+        dma("s", T.kx[p, 0:6, :], T.kid[2 * q, :], [], ["kx0_%d" % q])
+        dma("a", T.kx[p, 6:12, :], T.kid[2 * q + 1, :], [], ["kx1_%d" % q])
+
+    dma("a", T.lx[:], T.lett[:], [], ["lx"])
+    load(f)
+    dma("s", T.tbuf[:], T.tid[:], [], ["tbuf"])
+    for q in (n, m, me):
+        load(q)
     dma("s", T.tin[me], T.tid[2 * me:2 * me + 2, :], [], ["tin%d" % me])
-    dma("s", T.lin[me], T.lett[2 * me:2 * me + 2, :], [], ["lin%d" % me])
 
     def iota(key, out, pattern, base, mult):
         comp("g", [], [key], lambda: g.iota(out, pattern, base, mult, allow_small_or_imprecise_dtypes=True))
 
     comp("g", [], ["pi"], lambda: g.iota(T.pi[:], [[1, 1]], 0, 1))
     iota("imk", T.imk[:], [[1, 143]], 0, -1)
-    iota("e8i", T.e8i[0:8, :], [[1, 8], [0, 16]], 0, -1)
+    iota("frk", T.frk[:], [[0, 4], [64, 2], [1, 16]], 0, -1)
+    comp("g", [], ["expi"], lambda: g.iota(T.expi[:], [[20, 4], [1, 4]], 0, 0))
+    send("rt", "st", [(q, mine[cores[q]]) for q in others], lambda q: T.tbuf[q], T.tin[me], ["tbuf"])
 
-    V([], ["tz0"], lambda: v.memset(T.tw[:, 0:1024], 0.0))
-    act(["tz0"], ["tz1"], T.tw[:, 1024:1536], T.tw[:, 0:512])
-    V(["imk"], ["ih"], lambda: v.tensor_scalar(T.ih[:], T.imk[:, 0:128], 0.0, None, A.is_equal))
+    V([], ["tz0"], lambda: v.memset(T.tw[:, 0:512], 0.0))
+    act(["tz0"], ["tz1"], T.tw[:, 512:1024], T.tw[:, 0:512])
     V(["pi"], ["pci"], lambda: v.tensor_scalar(T.pci[:], T.pi[:], 15, None, A.bitwise_and))
-    V(["pi"], ["f1"], lambda: v.tensor_scalar(T.f1[:], T.pi[:], 15.0, 15.0, A.mult, A.add))
+    V(["pi"], ["sa"], lambda: v.tensor_scalar(T.sa[:], T.pi[:], 32.0, 128.0, A.is_lt, A.mult))
     V(["pci"], ["pcf"], lambda: v.tensor_copy(T.pcf[:], T.pci[:]))
+    V(["imk"], ["ih"], lambda: v.tensor_scalar(T.ih[:], T.imk[:, 0:128], 0.0, None, A.is_equal))
+    V(["pcf"], ["zz"], lambda: v.tensor_scalar(T.zz[:], T.pcf[:], 0.0, None, A.is_equal))
+    V(["pcf"], ["k16"], lambda: v.tensor_scalar(T.k16[:], T.pcf[:], -1.0, 15.0, A.mult, A.add))
+    V(["sa", "zz"], ["sk"], lambda: v.tensor_scalar(T.sk[:], T.sa[:], -16.0, T.zz[:], A.add, A.mult))
+    act(["lx"], ["lf"], T.lf[:], T.lx[:])
+    dma("s", T.lbuf[:], T.lf[:], ["lf"], ["lbuf"])
+    dma("s", T.lin[me], T.lf[32 * me:32 * me + 32, :], ["lf"], ["lin%d" % me])
+    tz = ["tz%d" % x for x in range(6)]
 
-    send("t", "st", lambda q: T.tbuf[q], T.tin[me], ["tbuf"])
-    send("l", "sl", lambda q: T.lbuf[q], T.lin[me], ["lbuf"])
+    code = float(M * me) - OFF
+    eng = topo.engines(core, cores[f])
+
+    def cast(q):
+        p = slice(32 * q, 32 * q + 32)
+        V(["kx0_%d" % q], ["kh0_%d" % q], lambda: v.tensor_copy(T.kh[p, :, 0:64], T.kx[p, 0:6, :]))
+        act(["kx1_%d" % q], ["kh1_%d" % q], T.kh[p, :, 64:128], T.kx[p, 6:12, :])
+
+    def turn(q):
+        p = slice(32 * q, 32 * q + 32)
+        comp("t", ["kh0_%d" % q, "kh1_%d" % q, "ih"], ["ps%d" % q],
+             [lambda b=b: pe.matmul(ps[q][:, b:192:6], T.kh[p, b, :], T.ih[p, p], True, True) for b in range(6)])
+
+    def leave(q, by):
+        o, i = T.ks[:, 192 * q:192 * q + 192], ps[q][:, 0:192]
+        if by == "v":
+            V(["ps%d" % q], ["ks%d" % q], lambda: v.tensor_scalar(o, i, code, None, A.add))
+        else:
+            comp("a", ["ps%d" % q], ["ks%d" % q], lambda: g.scalar.activation(o, i, F.Copy, bias=code))
+
+    def go(q):
+        send("rk", "sk%d" % q, [(q, eng)], lambda d: T.ks[:, 192 * d:192 * d + 192], T.kin[:, 192 * me:192 * me + 192],
+             ["ks%d" % q])
+
+    cast(f)
+    turn(f)
+    cast(n)
+    leave(f, "v")
+    go(f)
+    send("rl", "sl", [(d, mine[cores[d]]) for d in others], lambda d: T.lbuf[d], T.lin[me], ["lbuf"])
+    turn(n)
+    cast(m)
+    turn(m)
+    leave(n, "a")
+    go(n)
+    cast(me)
+    turn(me)
+    leave(m, "v")
+    go(m)
+    leave(me, "a")
+    act(["tz0"], ["tz3"], T.tw[:, 1536:2048], T.tw[:, 0:512])
     for q in others:
         arrive("rl%d" % q, got(q), ["lin%d" % q])
         arrive("rt%d" % q, got(q), ["tin%d" % q])
-    iota("frk", T.frk[:], [[0, 4], [64, 2], [1, 16]], 0, -1)
-    comp("g", [], ["expi"], lambda: g.iota(T.expi[:], [[1, 16]], 0, 0))
-    iota("kk", T.kk[:], [[1, 3]], 2, 0)
+        arrive("rk%d" % q, len(eng), ["kin%d" % q])
 
-    def cast(q, la, hf):
-        o = T.kh[:, 3 * hf:3 * hf + 3, 64 * la:64 * la + 64]
-        i = T.kx[:, 6 * la + 3 * hf:6 * la + 3 * hf + 3, :]
-        if q == "v":
-            V(["kx%d" % la], ["kh%d%d" % (la, hf)], lambda: v.tensor_copy(o, i))
-        else:
-            act(["kx%d" % la], ["kh%d%d" % (la, hf)], o, i)
-
-    for q, la, hf in (("v", 0, 0), ("a", 0, 1), ("v", 1, 0), ("a", 1, 1)):
-        cast(q, la, hf)
-    for hf in range(2):
-        for x in range(2):
-            comp("t", ["kh0%d" % hf, "kh1%d" % hf, "ih"], ["ps%d" % x],
-                 [lambda b=b: pe.matmul(ps[x][:, b:384:6], T.kh[:, b, :], T.ih[:, 64 * x:64 * x + 64], True, True)
-                  for b in range(3 * hf, 3 * hf + 3)])
-    code = float(M * me) - OFF
-    V(["ps0"], ["ks0"], lambda: v.tensor_scalar(T.ks[:, 0:384], ps[0][:, 0:384], code, None, A.add))
-    comp("a", ["ps1"], ["ks1"], lambda: g.scalar.activation(T.ks[:, 384:768], ps[1][:, 0:384], F.Copy, bias=code))
-    ksk = ["ks0", "ks1"]
-    eng = topo.engines(core, cores[near[0]])
-    ways = ([(near[0], eng[:len(eng) // 2]), (near[1], eng[len(eng) // 2:])], [(near[2], eng)])
-    deps("g", ksk, [])
-    for n, way in enumerate(ways):
-        g.remote_dma_fused([RemoteDMATransfer(dst_ids=[dst(cores[q])], dma_engine_mask=bits(e), remote_sem=T.sem["rk%d" % me],
-                                              src=T.ks[:, 192 * q:192 * q + 192], dst=T.kin[:, 192 * me:192 * me + 192])
-                            for q, e in way], local_sem=T.sem["sk%d" % n])
-        total["sk%d" % n] = len(eng)
-    for q in others:
-        arrive("rk%d" % q, len(eng) if q == near[2] else len(eng) // 2, ["kin%d" % q])
-
-    iota("tz2", T.tw[:, 1536:3072], [[0, 1536]], 0, 0)
-    tz = ["tz0", "tz1", "tz2"]
+    iota("e8i", T.e8i[0:8, :], [[1, 8], [0, 16]], 0, -1)
+    iota("tz5", T.tw[:, 2304:3072], [[0, 768]], 0, 0)
     iota("one", T.one[:], [[0, 128]], 1, 0)
     comp("g", ["one"], ["ib"], lambda: g.affine_select(T.ib[:], T.one[:], [[1, 128]], A.is_equal, 0.0, 0, -1))
     comp("g", ["one"], ["shb"], lambda: g.affine_select(T.shb[:], T.one[:], [[1, 128]], A.is_equal, 0.0, -3, -1))
+    iota("vt", T.vt[:], [[0, 32]], 0, 0)
+
+    def weight(j, k, x, w):
+        i = T.vt[:, 8 * j:8 * k]
+        comp("g", ["vt"], ["vt"], lambda: g.affine_select(i, i, [[0, k - j], [-16, 8]], A.not_equal, w, -x, 1))
+
+    for x in range(2):
+        weight(0, 1, 3 + x, 1.0)
+        weight(1, 4, x, 1.0)
+    weight(0, 1, 5, K17)
+    for j in range(1, 4):
+        weight(j, j + 1, 2, (j + 1) * K17)
+    iota("pdi", T.pdi[:], [[1, 2], [2, 64]], 0, -1)
 
     lins = ["lin%d" % q for q in range(4)]
     tins = ["tin%d" % q for q in range(4)]
-    for la in range(2):
-        dma("s", T.ht[32 * la:32 * la + 32, :], T.tin[:, 64 * la:64 * la + 64, :], tins, ["ht%d" % la])
-    dma("s", T.li[0:8, 0:1024], T.lin[:], lins, ["lia"])
-    dma("s", T.li[0:6, 1024:1040], T.lin[1:4, 0::64, :], lins, ["lib"])
-    dma("s", T.li[6:8, 1024:1040], T.lin[0, 0::64, :], lins, ["lic"])
+    for x in range(4):
+        dma("s", T.ht[16 * x:16 * x + 16, :], T.tin[:, 64 * (x % 2):64 * (x % 2) + 64, :], tins, ["ht%d" % x])
+    dma("s", T.lu[0:8, 0:1024], T.lin[:], lins, ["lua"])
+    dma("s", T.lu[0:6, 1024:1040], T.lin[1:4, 0::64, :], lins, ["lub"])
+    dma("s", T.lu[6:8, 1024:1040], T.lin[0, 0::64, :], lins, ["luc"])
+    lus = ["lua", "lub", "luc"]
 
-    def spread(q, ka, kb, va):
-        src, keys = (T.ks, ksk) if q == me else (T.kin, ["kin%d" % q])
+    def sums(q, ka, kb, va):
+        src, keys = (T.ks, ["ks%d" % me]) if q == me else (T.kin, ["kin%d" % q])
         c = 192 * q
         for k, a, b in ((ka, 0, va // 4), (kb, va // 4, 192)):
-            comp("t", keys + ["r%d" % n for n in range(4)], ["ps%d" % k],
-                 [lambda n=n: pe.matmul(ps[k][:, n:4 * (b - a):4], T["r%d" % n][:], src[:, c + a:c + b], True, True)
-                  for n in range(4)])
+            comp("t", keys + ["r%d" % x for x in range(4)], ["ps%d" % k],
+                 [lambda x=x: pe.matmul(ps[k][:, x:4 * (b - a):4], T["r%d" % x][:], src[:, c + a:c + b], True, True)
+                  for x in range(4)])
+
+    def copyv(q, ka, va):
         V(["ps%d" % ka], ["wa%d" % q], lambda: v.tensor_copy(T.win[:, M * q:M * q + va], ps[ka][:, 0:va]))
+
+    def copya(q, kb, va):
         act(["ps%d" % kb], ["wb%d" % q], T.win[:, M * q + va:M * q + M], ps[kb][:, 0:M - va])
 
-    for n in range(4):
-        V(["frk"], ["r%d" % n], lambda: v.tensor_scalar(T["r%d" % n][:], T.frk[:], float(-16 * n), None, A.is_equal))
-    spread(me, 4, 5, SA)
+    def block(q):
+        return T.win[:, M * q:M * q + M], T.tw[:, M * q:M * q + M], OFF - M * q
 
-    V(["e8i"], ["e8"], lambda: v.tensor_scalar(T.e8[0:8, :], T.e8i[0:8, :], 0.0, None, A.is_equal))
-    V(["imk", "f1"], ["f8"], lambda: v.tensor_scalar(T.f8[0:8, :], T.imk[0:8, :], T.f1[0:8, :], None, A.is_equal))
-    V(["imk", "f1"], ["f8s"],
-      lambda: v.tensor_scalar(T.f8s[0:8, :], T.imk[0:8, :], T.f1[0:8, :], 16.0, A.is_equal, A.mult))
-    V(["pcf"], ["k16"], lambda: v.tensor_scalar(T.k16[:], T.pcf[:], -1.0, 15.0, A.mult, A.add))
-    V(["pi"], ["poi"], lambda: v.tensor_scalar(T.poi[:], T.pi[:], 12, None, A.bitwise_and))
-    V(["pcf"], ["wab"], lambda: v.tensor_scalar(T.wab[:], T.pcf[:], 2.0, None, A.is_lt))
-    V(["pcf"], ["wf"], lambda: v.tensor_scalar(T.wf[:], T.pcf[:], 2.0, K17, A.is_equal, A.mult))
-    V(["pcf"], ["wg"], lambda: v.tensor_scalar(T.wg[:], T.pcf[:], 3.0, None, A.is_ge))
-    V(["pcf"], ["wh"], lambda: v.tensor_scalar(T.wh[:], T.pcf[:], 5.0, K17 - 1.0, A.is_ge, A.mult))
-    V(["poi"], ["own1"], lambda: v.tensor_scalar(T.own1[:], T.poi[:], 192.0, OFF, A.mult, A.add))
-    V(["imk", "k16"], ["t1h"], lambda: v.tensor_scalar(T.t1h[:], T.imk[:], T.k16[:], None, A.is_equal))
-    V(["kk", "wf", "wab"], ["wk"],
-      lambda: v.tensor_scalar(T.wk[:], T.kk[:], T.wf[:], T.wab[:], A.mult, A.add))
-    V(["wg", "wh"], ["w1"], lambda: v.tensor_tensor(T.w1[:], T.wg[:], T.wh[:], A.add))
-    V(["imk"], ["id"], lambda: v.tensor_scalar(T["id"][:], T.imk[:, 0:128], 0.0, None, A.is_equal))
-    V(["expi"], ["expu"], lambda: v.tensor_copy(T.expu[:], T.expi[:]))
-    for j, w in enumerate((T.wk[:, 0:1], T.w1[:], T.wk[:, 1:2], T.wk[:, 2:3])):
-        V(["imk", "k16", "w1", "wk"], ["vt%d" % j],
-          lambda: v.tensor_scalar(T.vt[:, 8 * j:8 * j + 8], T.imk[:, 15:143:16], T.k16[:], w, A.is_equal, A.mult))
+    def table1(q):
+        V(["wa%d" % q], ["n1_%d" % q],
+          lambda: v.tensor_scalar(T.n1u[:, 2 * q:2 * q + 1], T.win[:, M * q + 1:M * q + 2], block(q)[2], None, A.add))
 
-    for q, (ka, kb) in zip(near[:2], ((6, 7), (4, 5))):
-        spread(q, ka, kb, SB)
+    def table2(q, by="v"):
+        R, o, i = ["wa%d" % q, "wb%d" % q, "n1_%d" % q], T.n2u[:, 16 * q:16 * q + 16], T.n1u[:, 2 * q:2 * q + 1]
+        if by == "v":
+            V(R, ["n2_%d" % q], lambda: v.tensor_scalar(o, block(q)[0].indirect(i), block(q)[2], None, A.add))
+        else:
+            comp("a", R, ["n2_%d" % q], lambda: g.scalar.activation(o, block(q)[0].indirect(i), F.Copy, bias=block(q)[2]))
 
-    V(["lia"], ["lua"], lambda: v.tensor_copy(T.lu[0:8, 0:512], T.li[0:8, 0:512]))
-    act(["lia", "lib", "lic"], ["lub"], T.lu[0:8, 512:1040], T.li[0:8, 512:1040])
+    def table3(q, by="v"):
+        R, o, i = ["wa%d" % q, "wb%d" % q, "n2_%d" % q], T.nw[:, 64 * q:64 * q + 64], T.n2u[:, 20 * q:20 * q + 4]
+        if by == "v":
+            V(R, ["nw%d" % q], lambda: v.tensor_copy(o, block(q)[0].indirect(i)))
+        else:
+            act(R, ["nw%d" % q], o, block(q)[0].indirect(i))
 
-    hts = ["ht0", "ht1"]
-    V(hts, ["hb0"], lambda: v.tensor_copy(T.hb[0:64, 0:96], T.ht[0:64, :]))
-    comp("a", hts, ["hb2"], lambda: g.scalar.activation(T.hb[0:64, 192:288], T.ht[0:64, :], F.Sign))
-    V(hts + ["hb0"], ["hb1"], lambda: v.tensor_tensor(T.hb[0:64, 96:192], T.ht[0:64, :], T.hb[0:64, 0:96], A.subtract))
     tws = []
+
+    def idlists(q):
+        act(tws + ["n1_%d" % q], ["g1_%d" % q], T.g1[:, 16 * q:16 * q + 16], block(q)[1].indirect(T.n1u[:, 2 * q:2 * q + 1]))
+        act(tws + ["n2_%d" % q], ["g2_%d" % q], T.g2[:, 64 * q:64 * q + 64],
+            block(q)[1].indirect(T.n2u[:, 20 * q:20 * q + 4]))
+
+    for x in range(4):
+        V(["frk"], ["r%d" % x], lambda: v.tensor_scalar(T["r%d" % x][:], T.frk[:], float(-16 * x), None, A.is_equal))
+    sums(me, 4, 5, SA)
+    V(["expi"], ["expu"], lambda: v.tensor_copy(T.expu[:], T.expi[:]))
+    V(["imk"], ["llz"], lambda: v.tensor_scalar(T.ll[:], T.imk[:, 0:136], 0.0, None, A.mult))
+    V([], ["tz2"], lambda: v.memset(T.tw[:, 1024:1536], 0.0))
+    copyv(me, 4, SA)
+    copya(me, 5, SA)
+    comp("a", ["ih"], ["i16"], lambda: g.scalar.activation(T.i16[:], T.ih[:], F.Copy, scale=16.0))
+    V(["imk", "sk"], ["sh1"], lambda: v.tensor_scalar(T.sh1[:], T.imk[:, 0:128], 1.0, T.sk[:], A.add, A.is_equal))
+    V(["imk", "k16"], ["t1h"], lambda: v.tensor_scalar(T.t1h[:], T.imk[:], T.k16[:], None, A.is_equal))
+    deps("s", ["llz"], [])
+    dma("s", T.ll[:, 64:128], T.lin[:], lins, ["ll"])
+    table1(me)
+    table2(me)
+    table3(me)
+    V([], ["tz4"], lambda: v.memset(T.tw[:, 2048:2304], 0.0))
+    V(["e8i"], ["e8"], lambda: v.tensor_scalar(T.e8[0:8, :], T.e8i[0:8, :], 0.0, None, A.is_equal))
+
+    sums(f, 6, 7, SF)
+    copyv(f, 6, SF)
+    copya(f, 7, SF)
+    table1(f)
+
+    hts = ["ht%d" % x for x in range(4)]
+    act(hts, ["hb0"], T.hb[0:64, 0:192], T.ht[0:64, :])
+    comp("a", hts, ["hb2"], lambda: g.scalar.activation(T.hb[0:64, 384:576], T.ht[0:64, :], F.Sign))
+    V(hts + ["hb0"], ["hb1"], lambda: v.tensor_tensor(T.hb[0:64, 192:384], T.ht[0:64, :], T.hb[0:64, 0:192], A.subtract))
     for x in (0, 2, 1):
-        for s in range(4):
+        for s in range(2):
             deps("s", tz, [])
-            dma("s", T.tw[32 * s + x:32 * s + 32:16, :], T.hb[0:64, 96 * x:96 * x + 96], ["hb%d" % x], ["tw%d%d" % (x, s)])
+            dma("s", T.tw[64 * s + x:64 * s + 64:16, :], T.hb[0:64, 192 * x:192 * x + 192], ["hb%d" % x],
+                ["tw%d%d" % (x, s)])
             tws.append("tw%d%d" % (x, s))
 
-    def mask(k, a, b):
-        V(["ps%d" % k, "pcf"], ["em%d" % k],
-          lambda: v.tensor_scalar(T.em[:, a:b], ps[k][:, 0:b - a], T.pcf[:], None, A.is_equal))
+    def letters(k):
+        comp("t", ["lua", "e8"], ["ps%d" % (2 + k)],
+             [lambda s=s: pe.matmul(ps[2 + k][:, s:512:8], T.e8[0:8, :], T.lu[0:8, 128 * s + 64 * k:128 * s + 64 * k + 64],
+                                    True, True) for s in range(8)])
 
-    for k, a, b, uk in ((2, 0, 512, "lua"), (3, 512, 1024, "lub"), (0, 1024, 1040, "lub")):
-        comp("t", [uk, "e8"], ["ps%d" % k],
-             lambda: pe.matmul(ps[k][:, 0:b - a], T.e8[0:8, :], T.lu[0:8, a:b], True, True))
-    mask(2, 0, 512)
-    mask(0, 1024, 1040)
+    def mask(k):
+        V(["ps%d" % (2 + k), "pcf"], ["em%d" % k],
+          lambda: v.tensor_scalar(T.em[:, k:1024:2], ps[2 + k][:, 0:512], T.pcf[:], None, A.is_equal))
 
-    spread(near[2], 6, 7, SB)
-    calls = []
-    for i in range(16):
-        calls.append(lambda i=i: pe.matmul(ps[1][:, 0:64], T.f8s[0:8, 15 - i:143 - i], T.lu[0:8, i:1024:16], i == 0, False))
-        calls.append(lambda i=i: pe.matmul(ps[1][:, 0:64], T.f8[0:8, 15 - i:143 - i], T.lu[0:8, i + 1:i + 1010:16], False,
-                                           i == 15))
-    comp("t", ["lua", "lub", "f8", "f8s"], ["ps1"], calls)
+    def more():
+        comp("t", lus + ["e8"], ["ps0"],
+             [lambda e=e: pe.matmul(ps[0][:, 16 * e:16 * e + 16], T.e8[0:8, :], T.lu[0:8, 64 + e:64 + e + 961:64], True, True)
+              for e in range(3)])
+        comp("t", ["ll", "llz", "i16", "ih", "sh1"], ["ps1"],
+             [lambda: pe.matmul(ps[1][:, 0:64], T.i16[:], T.ll[:, 64:128], True, False),
+              lambda: pe.matmul(ps[1][:, 0:64], T.ih[:], T.ll[:, 65:129], False, False),
+              lambda: pe.matmul(ps[1][:, 0:64], T.sh1[:], T.ll[:, 1:65], False, True)])
+
+    ems = ["em0", "em1", "em2"]
+
+    sums(n, 4, 5, SN)
+    copyv(n, 4, SN)
+    copya(n, 5, SN)
+    letters(0)
+    letters(1)
+    more()
+    sums(m, 6, 7, SM)
+    table1(n)
+    mask(0)
+    table2(f, "a")
+    table3(f, "a")
+    mask(1)
     act(["ps1"], ["cu"], T.cu[:], ps[1][:, 0:64])
-
+    V(["ps0", "pcf"], ["em2"], lambda: v.tensor_scalar(T.em[:, 1024:1072], ps[0][:, 0:48], T.pcf[:], None, A.is_equal))
+    copyv(m, 6, SM)
+    copya(m, 7, SM)
+    table2(n)
+    table1(m)
+    table3(n)
+    table2(m)
+    table3(m)
+    for q in (me, f, n, m):
+        idlists(q)
+    act(["g1_%d" % q for q in range(4)] + ["expu"], ["g1e"], T.g1e[:], T.g1[:, 0:64].indirect(T.expu[:, 0:16]))
     wk = ["w%s%d" % (x, q) for q in range(4) for x in "ab"]
+    nws = ["nw%d" % q for q in range(4)]
+    g2s = ["g2_%d" % q for q in range(4)]
     win = T.win[:, 0:3072]
     twin = T.tw[:, 0:3072]
-    V(["wa%d" % q for q in range(4)], ["n1s"], lambda: v.tensor_reduce(T.n1s[:], T.win[:, 1::M], AxisListType.X, A.add))
-    V(["n1s", "own1"], ["n1u"], lambda: v.tensor_scalar(T.n1u[:, 0:1], T.n1s[:], T.own1[:], None, A.add))
-    V(wk + ["n1u"], ["n2u"], lambda: v.tensor_scalar(T.n2u[:], win.indirect(T.n1u[:, 0:1]), OFF, None, A.add))
-    V(wk + ["n2u"], ["nw"], lambda: v.tensor_copy(T.nw[:], win.indirect(T.n2u[:, 0:16])))
-
-    act(tws + ["n1u"], ["g1"], T.g1[:], twin.indirect(T.n1u[:, 0:1]))
-    act(["g1", "expu"], ["g1e"], T.g1e[:], T.g1[:, 0:16].indirect(T.expu[:, 0:16]))
-    act(tws + ["n2u"], ["g2"], T.g2[:], twin.indirect(T.n2u[:, 0:16]))
 
     portions = ((0, CUT), (CUT, 1024))
 
     def walk(p, h, w, lst, e, R):
         a, b = portions[h]
-        V(R + ["em2", "em0"] + (["em3"] if h else []), ["%s%d" % (p, h)],
-          lambda: v.tensor_tensor(T[p][:, a:b], w.indirect(lst[:, a // 16:b // 16]), T.em[:, a + e:b + e], A.mult))
+        V(R + ems, ["%s%d" % (p, h)],
+          lambda: v.tensor_tensor(T[p][:, a:b], w.indirect(lst[:, a // 16:b // 16]), T.em[:, a + 16 * e:b + 16 * e], A.mult))
 
     def nodes(bank, p, h):
         a, b = portions[h]
@@ -337,28 +417,25 @@ def rank_program(g, core, T, topo):
 
     def ids(q, rep, w, lst, a, b, R):
         key = "%s_%d" % (rep, a)
-        pieces[rep].append((key, a, b))
+        pieces[rep].append(key)
         i = w.indirect(lst[:, a // 16:b // 16])
         if q == "v":
             V(R, [key], lambda: v.tensor_copy(T[rep][:, a:b], i))
         else:
             act(R, [key], T[rep][:, a:b], i)
 
-    def value(rep, bank, n, j, lo, hi):
-        for c in range(lo, hi):
-            keys = [k for k, a, b in pieces[rep] if a < 128 * c + 128 and 128 * c < b]
-            comp("t", keys + ["vt%d" % (j + x) for x in range(n)], ["ps%d" % bank],
-                 lambda: pe.matmul(ps[bank][:, c:64 * n:8], T[rep][:, 128 * c:128 * c + 128], T.vt[:, 8 * j:8 * j + 8 * n],
-                                   True, True))
+    def value(rep, bank, x, j):
+        comp("t", pieces[rep] + ["vt"], ["ps%d" % bank],
+             [lambda s=s: pe.matmul(ps[bank][:, s:64 * x:8], T[rep][:, s:1024:8], T.vt[:, 8 * j:8 * j + 8 * x], True, True)
+              for s in range(8)])
 
-    walk("p3", 0, T.nw[:, 0:256], T.cu, 2, ["nw", "cu"])
-    nodes(4, "p3", 0)
-    comp("t", ["g1e", "g2", "shb", "ib"], ["ps0"],
+    walk("p3", 0, T.nw[:, 0:256], T.cu, 2, nws + ["cu"])
+    comp("t", ["g1e", "shb", "ib"] + g2s, ["ps0"],
          [lambda: pe.matmul(ps[0][:, 0:256], T.shb[:], T.g1e[:], True, False),
           lambda: pe.matmul(ps[0][:, 0:256], T.ib[:], T.g2[:], False, True)])
     act(["ps0"], ["g12"], T.g12[:], ps[0][:, 0:256])
-    mask(3, 512, 1024)
-    walk("p3", 1, T.nw[:, 0:256], T.cu, 2, ["nw", "cu"])
+    nodes(4, "p3", 0)
+    walk("p3", 1, T.nw[:, 0:256], T.cu, 2, nws + ["cu"])
     nodes(5, "p3", 1)
     for a in (0, 512):
         ids("a", "i12", T.g12[:, 0:256], T.cu, a, a + 512, ["g12", "cu"])
@@ -367,40 +444,36 @@ def rank_program(g, core, T, topo):
         walk("p4", h, win, T.n3u, 3, wk + ["n3u%d" % h])
         nodes(6 + h, "p4", h)
         ids("a", "i3", twin, T.n3u, portions[h][0], portions[h][1], tws + ["n3u%d" % h])
-    value("i12", 1, 2, 0, 0, 8)
-    value("i3", 3, 1, 2, 0, 8)
+    value("i12", 1, 2, 0)
+    value("i3", 3, 1, 2)
     lists(6, "n4u", 0)
     ids("v", "i4", twin, T.n4u, 0, CUT, tws + ["n4u0"])
     lists(7, "n4u", 1)
+    ids("v", "i4", twin, T.n4u, CUT, IV, tws + ["n4u1"])
+    ids("a", "i4", twin, T.n4u, IV, 1024, tws + ["n4u1"])
     V(["ps1"], ["b1"], lambda: v.tensor_copy(T.b1[:], ps[1][:, 64:128]))
-    ids("v", "i4", twin, T.n4u, CUT, 768, tws + ["n4u1"])
-    ids("a", "i4", twin, T.n4u, 768, 1024, tws + ["n4u1"])
     V(["ps1", "b1"], ["b2"], lambda: v.tensor_tensor(T.b2[:], ps[1][:, 0:64], T.b1[:], A.max))
-    value("i4", 0, 1, 3, 0, 8)
+    value("i4", 0, 1, 3)
     V(["ps3", "b2"], ["b3"], lambda: v.tensor_tensor(T.b3[:], ps[3][:, 0:64], T.b2[:], A.max))
     V(["ps0", "b3"], ["res"], lambda: v.tensor_tensor(T.res[:], ps[0][:, 0:64], T.b3[:], A.max))
+    V(["res"], ["rcv%d" % me],
+      lambda: v.tensor_copy(T.rcv[:, 16 * me:16 * me + 16], T.res[:, 16 * me:16 * me + 16]))
+    V(["pdi"], ["id"], lambda: v.tensor_scalar(T["id"][:], T.pdi[:], 0.0, None, A.is_equal))
 
-    deps("g", ["res"], [])
-    total["sr"] = 0
-    for way in ways:
-        g.remote_dma_fused([RemoteDMATransfer(dst_ids=[dst(cores[q])], dma_engine_mask=bits(e), remote_sem=T.sem["rr%d" % me],
-                                              src=T.res[:, 16 * q:16 * q + 16], dst=T.rcv[:, 16 * me:16 * me + 16])
-                            for q, e in way], local_sem=T.sem.sr)
-        total["sr"] += len(eng)
+    half = len(eng) // 2
+    for way in ([(f, eng)], [(n, eng[:half]), (m, eng[half:])]):
+        send("rr", "sr", way, lambda d: T.res[:, 16 * d:16 * d + 16], T.rcv[:, 16 * me:16 * me + 16], ["res"])
     for q in others:
-        arrive("rr%d" % q, len(eng) if q == near[2] else len(eng) // 2, ["rcv%d" % q])
-    for q, bank in zip([me] + near, (4, 5, 6, 7)):
-        i, key = (T.res, "res") if q == me else (T.rcv, "rcv%d" % q)
-        c = slice(128 * q, 128 * q + 128)
-        p = ps[bank][0:16, 0:128]
-        comp("t", [key, "id"], ["ps%d" % bank], lambda: pe.transpose(p, i[:, 16 * q:16 * q + 16], T["id"][:]))
-        V(["ps%d" % bank], ["rt%d" % q], lambda: v.tensor_scalar(T.rt[0:16, c], p, RND, RND, A.add, A.subtract))
-        V(["ps%d" % bank, "rt%d" % q], ["yi%d" % q],
-          lambda: v.tensor_tensor(T.yi[0:16, c], p, T.rt[0:16, c], A.subtract))
-        comp("a", ["rt%d" % q], ["yl%d" % q],
-             lambda: g.scalar.activation(T.yl[0:16, c], T.rt[0:16, c], F.Copy, scale=1.0 / K17))
-        dma("s", T.yid[2 * q:2 * q + 2, :], T.yi[0:16, c], ["yi%d" % q], ["oi%d" % q])
-        dma("a", T.ylen[2 * q:2 * q + 2, :], T.yl[0:16, c], ["yl%d" % q], ["ol%d" % q])
+        arrive("rr%d" % q, len(eng) if q == f else half, ["rcv%d" % q])
+    p = ps[5][0:64, 0:128]
+    comp("t", ["rcv%d" % q for q in range(4)] + ["id"], ["ps5"],
+         lambda: pe.matmul(p, T.rcv[:], T["id"][:], True, True))
+    V(["ps5"], ["rt"], lambda: v.tensor_scalar(T.rt[0:64, :], p, RND, RND, A.add, A.subtract))
+    V(["ps5", "rt"], ["yi"], lambda: v.tensor_tensor(T.yi[0:64, :], p, T.rt[0:64, :], A.subtract))
+    comp("a", ["rt"], ["yl"], lambda: g.scalar.activation(T.yl[0:64, :], T.rt[0:64, :], F.Copy, scale=1.0 / K17))
+    for hi in range(2):
+        dma("s", T.yid[:, 512 * hi:512 * hi + 512], T.yi[0:64, 64 * hi:64 * hi + 64], ["yi"], ["oi%d" % hi])
+        dma("a", T.ylen[:, 512 * hi:512 * hi + 512], T.yl[0:64, 64 * hi:64 * hi + 64], ["yl"], ["ol%d" % hi])
 
     for s in total:
         if seen.get(s, 0) < total[s]:

import numpy as np
from concourse.bass import DstId, RemoteDMATransfer
from concourse.mybir import AluOpType as A, ActivationFunctionType as F

NR = 4
M = 768
OFF = 1536.0
SA, SF, SN, SM = 320, 256, 256, 352
CUT = 480
IV = 832
K17 = 131072.0
RND = 12582912.0 * K17
HF = "float16"
BF = "bfloat16"
F32 = "float32"
I32 = "int32"
U16 = "uint16"


def sb(cols, dtype):
    return ("sbuf", [128] + (cols if isinstance(cols, list) else [cols]), dtype)


SCRATCH = {
    "lbuf": ("dram", [4, 128, 16], HF), "lin": ("dram", [4, 128, 16], HF),
    "tbuf": ("dram", [4, 128, 12], I32), "tin": ("dram", [4, 128, 12], I32),
    "lx": sb(64, I32), "lf": sb(64, HF), "kx": sb([12, 64], I32), "kh": sb([6, 128], HF),
    "ks": sb(768, HF), "kin": sb(768, HF),
    "win": sb(3072, F32), "tw": sb(3072, BF), "nw": sb(256, F32),
    "ht": sb(192, I32), "hb": sb(576, BF),
    "lu": sb(1040, HF), "ll": sb(136, HF), "em": sb(1072, BF),
    "pi": sb(1, I32), "pci": sb(1, I32),
    "pcf": sb(1, F32), "k16": sb(1, F32), "zz": sb(1, F32), "sa": sb(1, F32), "sk": sb(1, F32),
    "imk": sb(143, BF), "frk": sb(128, BF), "e8i": sb(128, BF), "pdi": sb(128, BF), "one": sb(128, BF),
    "expi": sb(16, I32), "expu": sb(16, U16),
    "e8": sb(128, HF), "ih": sb(128, HF), "i16": sb(128, HF), "sh1": sb(128, HF),
    "r0": sb(128, HF), "r1": sb(128, HF), "r2": sb(128, HF), "r3": sb(128, HF),
    "id": sb(128, F32), "ib": sb(128, BF), "shb": sb(128, BF), "t1h": sb(143, HF), "vt": sb(32, BF),
    "cu": sb(64, U16), "n1u": sb(8, U16), "n2u": sb(64, U16), "n3u": sb(64, U16), "n4u": sb(64, U16),
    "p3": sb(1024, HF), "p4": sb(1024, HF),
    "g1": sb(64, BF), "g1e": sb(256, BF), "g2": sb(256, BF), "g12": sb(256, BF),
    "i12": sb(1024, BF), "i3": sb(1024, BF), "i4": sb(1024, BF),
    "b1": sb(64, F32), "b2": sb(64, F32), "b3": sb(64, F32),
    "res": sb(64, F32), "rcv": sb(64, F32), "rt": sb(128, F32), "yl": sb(128, F32), "yi": sb(128, F32),
}
for _i in range(8):
    SCRATCH["ps%d" % _i] = ("psum", [128, 512], F32)
SEMAPHORES = (["cv", "ca", "ct", "cg", "sl", "st", "sr"]
              + ["%s%d" % (x, i) for x in ("sk", "rl", "rt", "rk", "rr") for i in range(NR)] + ["d%d" % i for i in range(48)])


def shares(topo, src, dsts):
    far = [d for d in dsts if not topo.mates(topo.chip(src), topo.chip(d))
           and not topo.same_plane(topo.chip(src), topo.chip(d))]
    order = far + [d for d in dsts if d not in far]
    out = {}
    at = 0
    for i, d in enumerate(order):
        e = topo.engines(src, d)
        n = len(e) // 2 if i == 0 else len(e) // 4
        out[d] = e[at:at + n]
        at += n
    return out


def bits(engines):
    return sum(1 << e for e in engines)


def rank_program(g, core, T, topo):
    me = T.rank_of(core)
    if me is None:
        return
    cores = list(T.cores)
    others = [q for q in range(NR) if q != me]
    mate = [q for q in others if topo.mates(topo.chip(core), topo.chip(cores[q]))]
    plane = [q for q in others if topo.same_plane(topo.chip(core), topo.chip(cores[q]))]
    order = [q for q in others if q not in mate + plane] + plane + mate
    f, n, m = order
    q_of = {"g": g, "v": g.vector, "a": g.scalar, "t": g.tensor, "s": g.sync}
    csem = {"g": "cg", "v": "cv", "a": "ca", "t": "ct"}
    total = {}
    waited = {}
    seen = {}
    lastw = {}
    reads = {}
    ndma = [0]

    def wait(q, evs):
        most = {}
        for s, x in evs:
            most[s] = max(x, most.get(s, 0))
        for s in most:
            if waited.get((q, s), 0) < most[s]:
                q_of[q].wait_ge(T.sem[s], most[s])
                waited[(q, s)] = most[s]
                seen[s] = max(seen.get(s, 0), most[s])

    def deps(q, R, W):
        own = csem.get(q)
        evs = []
        for k in R:
            evs += lastw.get(k, [])
        for k in W:
            evs += [e for e in lastw.get(k, []) + reads.get(k, []) if e[0] != own]
        wait(q, evs)

    def note(ev, R, W):
        for k in W:
            lastw[k] = [ev]
            reads[k] = []
        for k in R:
            reads.setdefault(k, []).append(ev)

    def comp(q, R, W, calls):
        deps(q, R, W)
        s = csem[q]
        for c in (calls if isinstance(calls, list) else [calls]):
            c().then_inc(T.sem[s], 1)
            total[s] = total.get(s, 0) + 1
        note((s, total[s]), R, W)

    def V(R, W, *calls):
        comp("v", R, W, list(calls))

    def act(R, W, o, i):
        comp("a", R, W, lambda: g.scalar.activation(o, i, F.Copy))

    def dma(q, out, in_, R, W):
        deps(q, R, W)
        s = "d%d" % ndma[0]
        ndma[0] += 1
        q_of[q].dma_start(out, in_).then_inc(T.sem[s], 16)
        total[s] = 16
        note((s, 16), R, W)

    def arrive(s, x, keys):
        total[s] = total.get(s, 0) + x
        for k in keys:
            lastw[k] = [(s, total[s])]

    def dst(d):
        rid, pid, _ = topo.addr(d)
        return DstId(rid=rid, pnc=pid)

    mine = shares(topo, core, [cores[q] for q in others])

    def send(rsem, lsem, way, src_of, out, R):
        deps("g", R, [])
        tr = [RemoteDMATransfer(dst_ids=[dst(cores[q])], dma_engine_mask=bits(e), remote_sem=T.sem["%s%d" % (rsem, me)],
                                src=src_of(q), dst=out) for q, e in way]
        g.remote_dma_fused(tr, local_sem=T.sem[lsem])
        total[lsem] = total.get(lsem, 0) + sum(len(e) for q, e in way)

    def got(q):
        return len(shares(topo, cores[q], [c for c in cores if c != cores[q]])[core])

    v = g.vector
    pe = g.tensor
    ps = [T["ps%d" % i] for i in range(8)]

    def load(q):
        p = slice(32 * q, 32 * q + 32)
        dma("s", T.kx[p, 0:6, :], T.kid[2 * q, :], [], ["kx0_%d" % q])
        dma("a", T.kx[p, 6:12, :], T.kid[2 * q + 1, :], [], ["kx1_%d" % q])

    dma("a", T.lx[:], T.lett[:], [], ["lx"])
    load(f)
    dma("s", T.tbuf[:], T.tid[:], [], ["tbuf"])
    for q in (n, m, me):
        load(q)
    dma("s", T.tin[me], T.tid[2 * me:2 * me + 2, :], [], ["tin%d" % me])

    def iota(key, out, pattern, base, mult):
        comp("g", [], [key], lambda: g.iota(out, pattern, base, mult, allow_small_or_imprecise_dtypes=True))

    comp("g", [], ["pi"], lambda: g.iota(T.pi[:], [[1, 1]], 0, 1))
    iota("imk", T.imk[:], [[1, 143]], 0, -1)
    iota("frk", T.frk[:], [[0, 4], [64, 2], [1, 16]], 0, -1)
    comp("g", [], ["expi"], lambda: g.iota(T.expi[:], [[20, 4], [1, 4]], 0, 0))
    send("rt", "st", [(q, mine[cores[q]]) for q in others], lambda q: T.tbuf[q], T.tin[me], ["tbuf"])

    V([], ["tz0"], lambda: v.memset(T.tw[:, 0:512], 0.0))
    act(["tz0"], ["tz1"], T.tw[:, 512:1024], T.tw[:, 0:512])
    V(["pi"], ["pci"], lambda: v.tensor_scalar(T.pci[:], T.pi[:], 15, None, A.bitwise_and))
    V(["pi"], ["sa"], lambda: v.tensor_scalar(T.sa[:], T.pi[:], 32.0, 128.0, A.is_lt, A.mult))
    V(["pci"], ["pcf"], lambda: v.tensor_copy(T.pcf[:], T.pci[:]))
    V(["imk"], ["ih"], lambda: v.tensor_scalar(T.ih[:], T.imk[:, 0:128], 0.0, None, A.is_equal))
    V(["pcf"], ["zz"], lambda: v.tensor_scalar(T.zz[:], T.pcf[:], 0.0, None, A.is_equal))
    V(["pcf"], ["k16"], lambda: v.tensor_scalar(T.k16[:], T.pcf[:], -1.0, 15.0, A.mult, A.add))
    V(["sa", "zz"], ["sk"], lambda: v.tensor_scalar(T.sk[:], T.sa[:], -16.0, T.zz[:], A.add, A.mult))
    act(["lx"], ["lf"], T.lf[:], T.lx[:])
    dma("s", T.lbuf[:], T.lf[:], ["lf"], ["lbuf"])
    dma("s", T.lin[me], T.lf[32 * me:32 * me + 32, :], ["lf"], ["lin%d" % me])
    tz = ["tz%d" % x for x in range(6)]

    code = float(M * me) - OFF
    eng = topo.engines(core, cores[f])

    def cast(q):
        p = slice(32 * q, 32 * q + 32)
        V(["kx0_%d" % q], ["kh0_%d" % q], lambda: v.tensor_copy(T.kh[p, :, 0:64], T.kx[p, 0:6, :]))
        act(["kx1_%d" % q], ["kh1_%d" % q], T.kh[p, :, 64:128], T.kx[p, 6:12, :])

    def turn(q):
        p = slice(32 * q, 32 * q + 32)
        comp("t", ["kh0_%d" % q, "kh1_%d" % q, "ih"], ["ps%d" % q],
             [lambda b=b: pe.matmul(ps[q][:, b:192:6], T.kh[p, b, :], T.ih[p, p], True, True) for b in range(6)])

    def leave(q, by):
        o, i = T.ks[:, 192 * q:192 * q + 192], ps[q][:, 0:192]
        if by == "v":
            V(["ps%d" % q], ["ks%d" % q], lambda: v.tensor_scalar(o, i, code, None, A.add))
        else:
            comp("a", ["ps%d" % q], ["ks%d" % q], lambda: g.scalar.activation(o, i, F.Copy, bias=code))

    def go(q):
        send("rk", "sk%d" % q, [(q, eng)], lambda d: T.ks[:, 192 * d:192 * d + 192], T.kin[:, 192 * me:192 * me + 192],
             ["ks%d" % q])

    cast(f)
    turn(f)
    cast(n)
    leave(f, "v")
    go(f)
    send("rl", "sl", [(d, mine[cores[d]]) for d in others], lambda d: T.lbuf[d], T.lin[me], ["lbuf"])
    turn(n)
    cast(m)
    turn(m)
    leave(n, "a")
    go(n)
    cast(me)
    turn(me)
    leave(m, "v")
    go(m)
    leave(me, "a")
    act(["tz0"], ["tz3"], T.tw[:, 1536:2048], T.tw[:, 0:512])
    for q in others:
        arrive("rl%d" % q, got(q), ["lin%d" % q])
        arrive("rt%d" % q, got(q), ["tin%d" % q])
        arrive("rk%d" % q, len(eng), ["kin%d" % q])

    iota("e8i", T.e8i[0:8, :], [[1, 8], [0, 16]], 0, -1)
    iota("tz5", T.tw[:, 2304:3072], [[0, 768]], 0, 0)
    iota("one", T.one[:], [[0, 128]], 1, 0)
    comp("g", ["one"], ["ib"], lambda: g.affine_select(T.ib[:], T.one[:], [[1, 128]], A.is_equal, 0.0, 0, -1))
    comp("g", ["one"], ["shb"], lambda: g.affine_select(T.shb[:], T.one[:], [[1, 128]], A.is_equal, 0.0, -3, -1))
    iota("vt", T.vt[:], [[0, 32]], 0, 0)

    def weight(j, k, x, w):
        i = T.vt[:, 8 * j:8 * k]
        comp("g", ["vt"], ["vt"], lambda: g.affine_select(i, i, [[0, k - j], [-16, 8]], A.not_equal, w, -x, 1))

    for x in range(2):
        weight(0, 1, 3 + x, 1.0)
        weight(1, 4, x, 1.0)
    weight(0, 1, 5, K17)
    for j in range(1, 4):
        weight(j, j + 1, 2, (j + 1) * K17)
    iota("pdi", T.pdi[:], [[1, 2], [2, 64]], 0, -1)

    lins = ["lin%d" % q for q in range(4)]
    tins = ["tin%d" % q for q in range(4)]
    for x in range(4):
        dma("s", T.ht[16 * x:16 * x + 16, :], T.tin[:, 64 * (x % 2):64 * (x % 2) + 64, :], tins, ["ht%d" % x])
    dma("s", T.lu[0:8, 0:1024], T.lin[:], lins, ["lua"])
    dma("s", T.lu[0:6, 1024:1040], T.lin[1:4, 0::64, :], lins, ["lub"])
    dma("s", T.lu[6:8, 1024:1040], T.lin[0, 0::64, :], lins, ["luc"])
    lus = ["lua", "lub", "luc"]

    def sums(q, ka, kb, va):
        src, keys = (T.ks, ["ks%d" % me]) if q == me else (T.kin, ["kin%d" % q])
        c = 192 * q
        for k, a, b in ((ka, 0, va // 4), (kb, va // 4, 192)):
            comp("t", keys + ["r%d" % x for x in range(4)], ["ps%d" % k],
                 [lambda x=x: pe.matmul(ps[k][:, x:4 * (b - a):4], T["r%d" % x][:], src[:, c + a:c + b], True, True)
                  for x in range(4)])

    def copyv(q, ka, va):
        V(["ps%d" % ka], ["wa%d" % q], lambda: v.tensor_copy(T.win[:, M * q:M * q + va], ps[ka][:, 0:va]))

    def copya(q, kb, va):
        act(["ps%d" % kb], ["wb%d" % q], T.win[:, M * q + va:M * q + M], ps[kb][:, 0:M - va])

    def block(q):
        return T.win[:, M * q:M * q + M], T.tw[:, M * q:M * q + M], OFF - M * q

    def table1(q):
        V(["wa%d" % q], ["n1_%d" % q],
          lambda: v.tensor_scalar(T.n1u[:, 2 * q:2 * q + 1], T.win[:, M * q + 1:M * q + 2], block(q)[2], None, A.add))

    def table2(q, by="v"):
        R, o, i = ["wa%d" % q, "wb%d" % q, "n1_%d" % q], T.n2u[:, 16 * q:16 * q + 16], T.n1u[:, 2 * q:2 * q + 1]
        if by == "v":
            V(R, ["n2_%d" % q], lambda: v.tensor_scalar(o, block(q)[0].indirect(i), block(q)[2], None, A.add))
        else:
            comp("a", R, ["n2_%d" % q], lambda: g.scalar.activation(o, block(q)[0].indirect(i), F.Copy, bias=block(q)[2]))

    def table3(q, by="v"):
        R, o, i = ["wa%d" % q, "wb%d" % q, "n2_%d" % q], T.nw[:, 64 * q:64 * q + 64], T.n2u[:, 20 * q:20 * q + 4]
        if by == "v":
            V(R, ["nw%d" % q], lambda: v.tensor_copy(o, block(q)[0].indirect(i)))
        else:
            act(R, ["nw%d" % q], o, block(q)[0].indirect(i))

    tws = []

    def idlists(q):
        act(tws + ["n1_%d" % q], ["g1_%d" % q], T.g1[:, 16 * q:16 * q + 16], block(q)[1].indirect(T.n1u[:, 2 * q:2 * q + 1]))
        act(tws + ["n2_%d" % q], ["g2_%d" % q], T.g2[:, 64 * q:64 * q + 64],
            block(q)[1].indirect(T.n2u[:, 20 * q:20 * q + 4]))

    for x in range(4):
        V(["frk"], ["r%d" % x], lambda: v.tensor_scalar(T["r%d" % x][:], T.frk[:], float(-16 * x), None, A.is_equal))
    sums(me, 4, 5, SA)
    V(["expi"], ["expu"], lambda: v.tensor_copy(T.expu[:], T.expi[:]))
    V(["imk"], ["llz"], lambda: v.tensor_scalar(T.ll[:], T.imk[:, 0:136], 0.0, None, A.mult))
    V([], ["tz2"], lambda: v.memset(T.tw[:, 1024:1536], 0.0))
    copyv(me, 4, SA)
    copya(me, 5, SA)
    comp("a", ["ih"], ["i16"], lambda: g.scalar.activation(T.i16[:], T.ih[:], F.Copy, scale=16.0))
    V(["imk", "sk"], ["sh1"], lambda: v.tensor_scalar(T.sh1[:], T.imk[:, 0:128], 1.0, T.sk[:], A.add, A.is_equal))
    V(["imk", "k16"], ["t1h"], lambda: v.tensor_scalar(T.t1h[:], T.imk[:], T.k16[:], None, A.is_equal))
    deps("s", ["llz"], [])
    dma("s", T.ll[:, 64:128], T.lin[:], lins, ["ll"])
    table1(me)
    table2(me)
    table3(me)
    V([], ["tz4"], lambda: v.memset(T.tw[:, 2048:2304], 0.0))
    V(["e8i"], ["e8"], lambda: v.tensor_scalar(T.e8[0:8, :], T.e8i[0:8, :], 0.0, None, A.is_equal))

    sums(f, 6, 7, SF)
    copyv(f, 6, SF)
    copya(f, 7, SF)
    table1(f)

    hts = ["ht%d" % x for x in range(4)]
    act(hts, ["hb0"], T.hb[0:64, 0:192], T.ht[0:64, :])
    comp("a", hts, ["hb2"], lambda: g.scalar.activation(T.hb[0:64, 384:576], T.ht[0:64, :], F.Sign))
    V(hts + ["hb0"], ["hb1"], lambda: v.tensor_tensor(T.hb[0:64, 192:384], T.ht[0:64, :], T.hb[0:64, 0:192], A.subtract))
    for x in (0, 2, 1):
        for s in range(2):
            deps("s", tz, [])
            dma("s", T.tw[64 * s + x:64 * s + 64:16, :], T.hb[0:64, 192 * x:192 * x + 192], ["hb%d" % x],
                ["tw%d%d" % (x, s)])
            tws.append("tw%d%d" % (x, s))

    def letters(k):
        comp("t", ["lua", "e8"], ["ps%d" % (2 + k)],
             [lambda s=s: pe.matmul(ps[2 + k][:, s:512:8], T.e8[0:8, :], T.lu[0:8, 128 * s + 64 * k:128 * s + 64 * k + 64],
                                    True, True) for s in range(8)])

    def mask(k):
        V(["ps%d" % (2 + k), "pcf"], ["em%d" % k],
          lambda: v.tensor_scalar(T.em[:, k:1024:2], ps[2 + k][:, 0:512], T.pcf[:], None, A.is_equal))

    def more():
        comp("t", lus + ["e8"], ["ps0"],
             [lambda e=e: pe.matmul(ps[0][:, 16 * e:16 * e + 16], T.e8[0:8, :], T.lu[0:8, 64 + e:64 + e + 961:64], True, True)
              for e in range(3)])
        comp("t", ["ll", "llz", "i16", "ih", "sh1"], ["ps1"],
             [lambda: pe.matmul(ps[1][:, 0:64], T.i16[:], T.ll[:, 64:128], True, False),
              lambda: pe.matmul(ps[1][:, 0:64], T.ih[:], T.ll[:, 65:129], False, False),
              lambda: pe.matmul(ps[1][:, 0:64], T.sh1[:], T.ll[:, 1:65], False, True)])

    ems = ["em0", "em1", "em2"]

    sums(n, 4, 5, SN)
    copyv(n, 4, SN)
    copya(n, 5, SN)
    letters(0)
    letters(1)
    more()
    sums(m, 6, 7, SM)
    table1(n)
    mask(0)
    table2(f, "a")
    table3(f, "a")
    mask(1)
    act(["ps1"], ["cu"], T.cu[:], ps[1][:, 0:64])
    V(["ps0", "pcf"], ["em2"], lambda: v.tensor_scalar(T.em[:, 1024:1072], ps[0][:, 0:48], T.pcf[:], None, A.is_equal))
    copyv(m, 6, SM)
    copya(m, 7, SM)
    table2(n)
    table1(m)
    table3(n)
    table2(m)
    table3(m)
    for q in (me, f, n, m):
        idlists(q)
    act(["g1_%d" % q for q in range(4)] + ["expu"], ["g1e"], T.g1e[:], T.g1[:, 0:64].indirect(T.expu[:, 0:16]))
    wk = ["w%s%d" % (x, q) for q in range(4) for x in "ab"]
    nws = ["nw%d" % q for q in range(4)]
    g2s = ["g2_%d" % q for q in range(4)]
    win = T.win[:, 0:3072]
    twin = T.tw[:, 0:3072]

    portions = ((0, CUT), (CUT, 1024))

    def walk(p, h, w, lst, e, R):
        a, b = portions[h]
        V(R + ems, ["%s%d" % (p, h)],
          lambda: v.tensor_tensor(T[p][:, a:b], w.indirect(lst[:, a // 16:b // 16]), T.em[:, a + 16 * e:b + 16 * e], A.mult))

    def nodes(bank, p, h):
        a, b = portions[h]
        comp("t", ["%s%d" % (p, h), "t1h"], ["ps%d" % bank],
             [lambda i=i: pe.matmul(ps[bank][:, 0:(b - a) // 16], T.t1h[:, 15 - i:143 - i], T[p][:, a + i:b:16], i == 0,
                                    i == 15) for i in range(16)])

    def lists(bank, nm, h):
        a, b = portions[h]
        V(["ps%d" % bank], ["%s%d" % (nm, h)],
          lambda: v.tensor_scalar(T[nm][:, a // 16:b // 16], ps[bank][:, 0:(b - a) // 16], OFF, None, A.add))

    pieces = {"i12": [], "i3": [], "i4": []}

    def ids(q, rep, w, lst, a, b, R):
        key = "%s_%d" % (rep, a)
        pieces[rep].append(key)
        i = w.indirect(lst[:, a // 16:b // 16])
        if q == "v":
            V(R, [key], lambda: v.tensor_copy(T[rep][:, a:b], i))
        else:
            act(R, [key], T[rep][:, a:b], i)

    def value(rep, bank, x, j):
        comp("t", pieces[rep] + ["vt"], ["ps%d" % bank],
             [lambda s=s: pe.matmul(ps[bank][:, s:64 * x:8], T[rep][:, s:1024:8], T.vt[:, 8 * j:8 * j + 8 * x], True, True)
              for s in range(8)])

    walk("p3", 0, T.nw[:, 0:256], T.cu, 2, nws + ["cu"])
    comp("t", ["g1e", "shb", "ib"] + g2s, ["ps0"],
         [lambda: pe.matmul(ps[0][:, 0:256], T.shb[:], T.g1e[:], True, False),
          lambda: pe.matmul(ps[0][:, 0:256], T.ib[:], T.g2[:], False, True)])
    act(["ps0"], ["g12"], T.g12[:], ps[0][:, 0:256])
    nodes(4, "p3", 0)
    walk("p3", 1, T.nw[:, 0:256], T.cu, 2, nws + ["cu"])
    nodes(5, "p3", 1)
    for a in (0, 512):
        ids("a", "i12", T.g12[:, 0:256], T.cu, a, a + 512, ["g12", "cu"])
    for h in range(2):
        lists(4 + h, "n3u", h)
        walk("p4", h, win, T.n3u, 3, wk + ["n3u%d" % h])
        nodes(6 + h, "p4", h)
        ids("a", "i3", twin, T.n3u, portions[h][0], portions[h][1], tws + ["n3u%d" % h])
    value("i12", 1, 2, 0)
    value("i3", 3, 1, 2)
    lists(6, "n4u", 0)
    ids("v", "i4", twin, T.n4u, 0, CUT, tws + ["n4u0"])
    lists(7, "n4u", 1)
    ids("v", "i4", twin, T.n4u, CUT, IV, tws + ["n4u1"])
    ids("a", "i4", twin, T.n4u, IV, 1024, tws + ["n4u1"])
    V(["ps1"], ["b1"], lambda: v.tensor_copy(T.b1[:], ps[1][:, 64:128]))
    V(["ps1", "b1"], ["b2"], lambda: v.tensor_tensor(T.b2[:], ps[1][:, 0:64], T.b1[:], A.max))
    value("i4", 0, 1, 3)
    V(["ps3", "b2"], ["b3"], lambda: v.tensor_tensor(T.b3[:], ps[3][:, 0:64], T.b2[:], A.max))
    V(["ps0", "b3"], ["res"], lambda: v.tensor_tensor(T.res[:], ps[0][:, 0:64], T.b3[:], A.max))
    V(["res"], ["rcv%d" % me],
      lambda: v.tensor_copy(T.rcv[:, 16 * me:16 * me + 16], T.res[:, 16 * me:16 * me + 16]))
    V(["pdi"], ["id"], lambda: v.tensor_scalar(T["id"][:], T.pdi[:], 0.0, None, A.is_equal))

    half = len(eng) // 2
    for way in ([(f, eng)], [(n, eng[:half]), (m, eng[half:])]):
        send("rr", "sr", way, lambda d: T.res[:, 16 * d:16 * d + 16], T.rcv[:, 16 * me:16 * me + 16], ["res"])
    for q in others:
        arrive("rr%d" % q, len(eng) if q == f else half, ["rcv%d" % q])
    p = ps[5][0:64, 0:128]
    comp("t", ["rcv%d" % q for q in range(4)] + ["id"], ["ps5"],
         lambda: pe.matmul(p, T.rcv[:], T["id"][:], True, True))
    V(["ps5"], ["rt"], lambda: v.tensor_scalar(T.rt[0:64, :], p, RND, RND, A.add, A.subtract))
    V(["ps5", "rt"], ["yi"], lambda: v.tensor_tensor(T.yi[0:64, :], p, T.rt[0:64, :], A.subtract))
    comp("a", ["rt"], ["yl"], lambda: g.scalar.activation(T.yl[0:64, :], T.rt[0:64, :], F.Copy, scale=1.0 / K17))
    for hi in range(2):
        dma("s", T.yid[:, 512 * hi:512 * hi + 512], T.yi[0:64, 64 * hi:64 * hi + 64], ["yi"], ["oi%d" % hi])
        dma("a", T.ylen[:, 512 * hi:512 * hi + 512], T.yl[0:64, 64 * hi:64 * hi + 64], ["yl"], ["ol%d" % hi])

    for s in total:
        if seen.get(s, 0) < total[s]:
            wait("g", [(s, total[s])])
